import numpy as np
import ml_dtypes


def mxq(x, axis, fmt="e4m3"):
    dtype, down = {"e4m3": (ml_dtypes.float8_e4m3fn, 7), "e5m2": (ml_dtypes.float8_e5m2, 14)}[fmt]
    v = np.moveaxis(np.asarray(x, np.float32).astype(ml_dtypes.bfloat16).astype(np.float64), axis, -1)
    blocks = v.reshape(v.shape[:-1] + (-1, 32))
    amax = np.abs(blocks).max(-1, keepdims=True)
    byte = np.maximum(np.where(amax > 0, np.frexp(amax)[1] - 1 + 127, 0) - down, 1)
    scale = np.exp2(byte - 127.0)
    codes = (blocks / scale).astype(np.float32).astype(dtype).astype(np.float64)
    return np.moveaxis((codes * scale).reshape(v.shape), -1, axis)


WIDE = False


def mx_kscale(k):
    if not WIDE:
        return np.ones(k)
    levels = np.array([10, -10, 5, -5, 0])
    if k % 512:
        return np.exp2(np.random.permutation(np.resize(levels, k // 32))).repeat(32)
    a = np.empty((k // 512, 16))
    for p in range(k // 512):
        a[p, :8] = np.random.permutation(np.resize(levels, 8))
        for g in range(8):
            far = levels[np.abs(levels - a[p, g]) >= 10]
            a[p, g + 8] = far[np.random.randint(len(far))]
    return np.exp2(a.ravel()).repeat(32)


def f64(x):
    return np.asarray(x).astype(np.float64)


def striped(idx):
    return np.tile(idx.reshape(-1, 16).T, (8, 1)).astype(np.uint16)


def unstriped(offs):
    return offs[:16].T.reshape(-1).astype(np.int64)


def striped8(idx):
    return np.concatenate([x.reshape(-1, 16).T for x in idx]).astype(np.uint16)


def runs(offs, k):
    lists = np.stack([offs[16 * r : 16 * r + 16].T.reshape(-1) for r in range(8)]).astype(np.int64)
    return lists[np.arange(k) % 512 // 64]


def pack_weight(w):
    k, n = w.shape
    w = f64(np.asarray(w, np.float32).astype(ml_dtypes.bfloat16)).reshape(k // 32, 32, n)
    amax = np.abs(w).max(1)
    byte = np.clip(np.where(amax > 0, np.frexp(amax)[1] - 1 + 127 - 7, 1), 1, 254)
    scaled = (w * np.exp2(127.0 - byte)[:, None, :]).reshape(k, n).astype(np.float32)
    words = np.ascontiguousarray(scaled.reshape(k // 512, 128, 4, n).transpose(0, 1, 3, 2)).astype(ml_dtypes.float8_e4m3fn).view(np.uint8)
    return words, np.ascontiguousarray(byte.astype(np.uint8).reshape(k // 512, 16, n))


def unpack_weight(words, scales):
    g, p, n, _ = words.shape
    vals = np.ascontiguousarray(words).view(ml_dtypes.float8_e4m3fn).astype(np.float64) * np.repeat(np.exp2(scales.astype(np.float64) - 127.0), 8, axis=1)[..., None]
    return vals.transpose(0, 1, 3, 2).reshape(g * 512, n)


K, T, S, V, N = 512, 2048, 512, 256, 512


def setup_inputs():
    n = np.random.standard_normal
    s = mx_kscale(K)[:, None]
    packed_xT = pack_weight(n((K, T)) * s)
    return {
        "x_words": packed_xT[0],
        "x_scales": packed_xT[1],
        "w1": (n((K, N)) / np.sqrt(K) / s).astype(np.float32),
        "w2": (n((K, N)) / np.sqrt(K) / s).astype(np.float32),
        "sh": np.repeat(np.random.uniform(0.2, 0.8, (8, V)), 64, axis=0).astype(np.float32),
        "offs": striped(np.random.permutation(T)[:S]),
        "acc_l": striped8(np.stack([np.random.permutation(S)[:V] for _ in range(8)])),
    }


def reference(x_words, x_scales, w1, w2, sh, offs, acc_l):
    xq = unpack_weight(x_words, x_scales)[:, unstriped(offs)]
    y = mxq(f64(w1), 0, "e4m3").T @ xq
    yt = y[np.arange(N)[:, None], runs(acc_l, N)]
    e = mxq(f64(w2), 0, "e4m3").T @ xq
    q = yt + f64(sh) * (e[np.arange(N)[:, None], runs(acc_l, N)] - yt)
    out = y.copy()
    out[np.arange(N)[:, None], runs(acc_l, N)] = q
    return out

@@ -1,0 +1,142 @@
+from contextlib import ExitStack
+
+import concourse.mybir as mybir
+
+K, T, S, V, N = 512, 2048, 512, 256, 512
+FLOPS = 2 * 2 * K * N * S
+BYTES = 128 * T * 4 + 16 * T + 2 * K * N * 4 + 8 * V * 4 + N * S * 4
+
+F32 = mybir.dt.float32
+BF16 = mybir.dt.bfloat16
+I32 = mybir.dt.int32
+U32 = mybir.dt.uint32
+U16 = mybir.dt.uint16
+U8 = mybir.dt.uint8
+FP8X4 = mybir.dt.float8_e4m3fn_x4
+MULT = mybir.AluOpType.mult
+ADD = mybir.AluOpType.add
+COPY = mybir.ActivationFunctionType.Copy
+
+P = 128
+PACK = 4
+TILES = N // P
+PAIR = 2
+HALF = S // 2
+
+
+def tile_picked_specacc_none_p_kernel(tc, x_words, x_scales, w1, w2, sh, offs, acc_l, out):
+    nc = tc.nc
+    with ExitStack() as ctx:
+        keep = ctx.enter_context(tc.tile_pool(name="keep", bufs=1))
+        reuse = ctx.enter_context(tc.tile_pool(name="reuse", bufs=1))
+        psum = ctx.enter_context(tc.psum_pool(name="psum", bufs=8))
+
+        offs_t = keep.tile([P, S // 16], U16, name="offs_t")
+        acc_t = keep.tile([P, V // 16], U16, name="acc_t")
+        scale_win = keep.tile([P, T], U8, name="scale_win", align_bytes=64)
+        word_win = keep.tile([P, T], I32, name="word_win", align_bytes=64)
+        w1_raw = keep.tile([P, PACK, N], F32, name="w1_raw", align_bytes=64)
+        w2_raw = keep.tile([P, PACK, N], F32, name="w2_raw", align_bytes=64)
+        share = keep.tile([P, V], F32, name="share", align_bytes=64)
+        rest = keep.tile([P, V], F32, name="rest", align_bytes=64)
+        x_codes = [keep.tile([P, HALF], U32, name=f"x_codes{h}", align_bytes=64) for h in range(2)]
+        x_plane = keep.tile([P, S], U8, name="x_plane", align_bytes=64)
+
+        nc.vector.memset(scale_win[:].bitcast(I32), 0)
+        nc.sync.dma_start(offs_t[:], offs)
+        nc.sync.dma_start(w1_raw[:], w1.rearrange("(p j) n -> p j n", j=PACK))
+        scale_rows = x_scales[0].bitcast(I32)
+        for q in range(4):
+            nc.sync.dma_start(scale_win[32 * q : 32 * q + 4, :].bitcast(I32), scale_rows[4 * q : 4 * q + 4, :])
+        nc.sync.dma_start(word_win[:], x_words[0].rearrange("p n t -> p (n t)").bitcast(I32))
+        nc.sync.dma_start(acc_t[:], acc_l)
+        nc.sync.dma_start(share[:], sh.rearrange("(p t) v -> p t v", t=TILES)[:, 0, :])
+        nc.sync.dma_start(w2_raw[:], w2.rearrange("(p j) n -> p j n", j=PACK))
+
+        def round_pair(copy, raw, pair, grouped):
+            src = raw[:].rearrange("p j (m t) -> p m j t", t=TILES)[:, :, :, PAIR * pair : PAIR * pair + PAIR]
+            copy(grouped[:].rearrange("p (t m j) -> p m j t", t=PAIR, j=PACK), src)
+            return grouped
+
+        def quantize_pair(grouped, name):
+            codes = keep.tile([P, PAIR * P], U32, name=name + "_codes", align_bytes=64)
+            plane = keep.tile([P, PAIR * P], U8, name=name + "_plane", align_bytes=64)
+            nc.vector.quantize_mx(out=codes[:].bitcast(FP8X4), scales=plane[:], in_=grouped[:])
+            return codes, plane
+
+        def half_product(weights, t, h, acc):
+            codes, plane = weights[t // PAIR]
+            m_cols = slice((t % PAIR) * P, (t % PAIR + 1) * P)
+            nc.tensor.matmul_mx(
+                out=acc,
+                lhsT=codes[:, m_cols].bitcast(FP8X4),
+                lhsT_scale=plane[:, m_cols],
+                rhs=x_codes[h][:].bitcast(FP8X4),
+                rhs_scale=x_plane[:, h * HALF : (h + 1) * HALF],
+                start=True,
+                stop=True,
+            )
+
+        def product(weights, t, dst):
+            acc = psum.tile([P, S], F32, name="acc")
+            for h in range(2):
+                half_product(weights, t, h, acc[:, h * HALF : (h + 1) * HALF])
+            nc.scalar.copy(dst[:], acc[:])
+
+        def staging(pool, name, **where):
+            return pool.tile([P, PAIR * P * PACK], BF16, name=name, align_bytes=64, **where)
+
+        nc.vector.tensor_copy(x_plane[:], scale_win[:].indirect(offs_t[:]))
+        g1 = [round_pair(nc.vector.tensor_copy, w1_raw, 0, staging(keep, "w1_lo")), round_pair(nc.scalar.copy, w1_raw, 1, staging(keep, "w1_hi"))]
+        q1 = [quantize_pair(g1[0], "w1_lo"), quantize_pair(g1[1], "w1_hi")]
+        for h in range(2):
+            nc.vector.tensor_copy(
+                x_codes[h][:],
+                word_win[:].bitcast(U32).indirect(offs_t[:, h * HALF // 16 : (h + 1) * HALF // 16]),
+            )
+        nc.gpsimd.tensor_scalar(rest[:], share[:], -1.0, 1.0, MULT, ADD)
+
+        y = [keep.tile([P, S], F32, name=f"y{t}", align_bytes=64) for t in range(TILES)]
+        e = [keep.tile([P, S], F32, name=f"e{t}", align_bytes=64) for t in range(TILES)]
+        kept = {t: keep.tile([P, V], F32, name=f"kept{t}", align_bytes=64) for t in (0, 2, 3)}
+        drafted = [keep.tile([P, V], F32, name=f"drafted{t}", align_bytes=64) for t in range(TILES)]
+        out_t = out.rearrange("(p t) s -> p t s", t=TILES)
+
+        def gather_y(t):
+            nc.vector.tensor_tensor(kept[t][:], y[t][:].indirect(acc_t[:]), rest[:], MULT)
+
+        def gather_e(t):
+            nc.vector.tensor_tensor(drafted[t][:], e[t][:].indirect(acc_t[:]), share[:], MULT)
+
+        def put(t):
+            nc.vector.tensor_tensor(y[t][:].indirect(acc_t[:]), kept[t][:], drafted[t][:], ADD)
+            nc.sync.dma_start(out_t[:, t, :], y[t][:])
+
+        for h in range(2):
+            acc = psum.tile([P, S], F32, name="acc")
+            half_product(q1, 0, h, acc[:, 0:HALF])
+            nc.scalar.copy(y[0][:, h * HALF : (h + 1) * HALF], acc[:, 0:HALF])
+        product(q1, 1, y[1])
+        product(q1, 2, y[2])
+        gather_y(0)
+        g2_lo = round_pair(nc.vector.tensor_copy, w2_raw, 0, staging(reuse, "w2_lo", offset=0))
+        q2 = [quantize_pair(g2_lo, "w2_lo")]
+        kept[1] = reuse.tile([P, V], F32, name="kept1", align_bytes=64, offset=0)
+        gather_y(1)
+        product(q1, 3, y[3])
+        product(q2, 0, e[0])
+        product(q2, 1, e[1])
+        g2_hi = round_pair(nc.scalar.copy, w2_raw, 1, staging(reuse, "w2_hi", offset=V * 4))
+        gather_y(2)
+        gather_y(3)
+        gather_e(0)
+        gather_e(1)
+        put(0)
+        q2.append(quantize_pair(g2_hi, "w2_hi"))
+        product(q2, 2, e[2])
+        product(q2, 3, e[3])
+        put(1)
+        gather_e(2)
+        gather_e(3)
+        put(2)
+        put(3)

@@ -28,7 +28,7 @@ def tile_picked_specacc_none_p_kernel(tc, x_words, x_scales, w1, w2, sh, offs, a
     nc = tc.nc
     with ExitStack() as ctx:
         keep = ctx.enter_context(tc.tile_pool(name="keep", bufs=1))
-        reuse = ctx.enter_context(tc.tile_pool(name="reuse", bufs=1))
+        late = ctx.enter_context(tc.tile_pool(name="late", bufs=1))
         psum = ctx.enter_context(tc.psum_pool(name="psum", bufs=8))
 
         offs_t = keep.tile([P, S // 16], U16, name="offs_t")
@@ -36,71 +36,83 @@ def tile_picked_specacc_none_p_kernel(tc, x_words, x_scales, w1, w2, sh, offs, a
         scale_win = keep.tile([P, T], U8, name="scale_win", align_bytes=64)
         word_win = keep.tile([P, T], I32, name="word_win", align_bytes=64)
         w1_raw = keep.tile([P, PACK, N], F32, name="w1_raw", align_bytes=64)
-        w2_raw = keep.tile([P, PACK, N], F32, name="w2_raw", align_bytes=64)
+        w2_early = keep.tile([P, PACK, N // 2], F32, name="w2_early", align_bytes=64)
+        w2_late = late.tile([P, PACK, N // 2], F32, name="w2_late", align_bytes=64, offset=0)
         share = keep.tile([P, V], F32, name="share", align_bytes=64)
         rest = keep.tile([P, V], F32, name="rest", align_bytes=64)
         x_codes = [keep.tile([P, HALF], U32, name=f"x_codes{h}", align_bytes=64) for h in range(2)]
         x_plane = keep.tile([P, S], U8, name="x_plane", align_bytes=64)
+        w1_bf = keep.tile([P, N * PACK], BF16, name="w1_bf", align_bytes=64)
+        w2_bf = keep.tile([P, N * PACK], BF16, name="w2_bf", align_bytes=64)
 
         nc.vector.memset(scale_win[:].bitcast(I32), 0)
         nc.sync.dma_start(offs_t[:], offs)
         nc.sync.dma_start(w1_raw[:], w1.rearrange("(p j) n -> p j n", j=PACK))
         scale_rows = x_scales[0].bitcast(I32)
-        for q in range(4):
-            nc.sync.dma_start(scale_win[32 * q : 32 * q + 4, :].bitcast(I32), scale_rows[4 * q : 4 * q + 4, :])
+        for r in range(4):
+            nc.sync.dma_start(scale_win[r:P:32, :].bitcast(I32), scale_rows[r:16:4, :])
         nc.sync.dma_start(word_win[:], x_words[0].rearrange("p n t -> p (n t)").bitcast(I32))
-        nc.sync.dma_start(acc_t[:], acc_l)
         nc.sync.dma_start(share[:], sh.rearrange("(p t) v -> p t v", t=TILES)[:, 0, :])
-        nc.sync.dma_start(w2_raw[:], w2.rearrange("(p j) n -> p j n", j=PACK))
+        w2_rows = w2.rearrange("(p j) n -> p j n", j=PACK)
+        nc.sync.dma_start(w2_early[:], w2_rows[:, :, 0 : N // 2])
+        nc.sync.dma_start(w2_late[:], w2_rows[:, :, N // 2 : N])
+        nc.sync.dma_start(acc_t[:], acc_l)
 
-        def round_pair(copy, raw, pair, grouped):
-            src = raw[:].rearrange("p j (m t) -> p m j t", t=TILES)[:, :, :, PAIR * pair : PAIR * pair + PAIR]
-            copy(grouped[:].rearrange("p (t m j) -> p m j t", t=PAIR, j=PACK), src)
-            return grouped
+        def round_rows(copy, raw, first, grouped):
+            count = raw.shape[2] // TILES
+            dst = grouped[:].rearrange("p (t m j) -> p m j t", t=TILES, j=PACK)[:, first : first + count]
+            copy(dst, raw.rearrange("p j (m t) -> p m j t", t=TILES))
 
-        def quantize_pair(grouped, name):
-            codes = keep.tile([P, PAIR * P], U32, name=name + "_codes", align_bytes=64)
-            plane = keep.tile([P, PAIR * P], U8, name=name + "_plane", align_bytes=64)
-            nc.vector.quantize_mx(out=codes[:].bitcast(FP8X4), scales=plane[:], in_=grouped[:])
-            return codes, plane
+        def quantize(grouped, first, count, name):
+            codes = keep.tile([P, count * P], U32, name=name + "_codes", align_bytes=64)
+            plane = keep.tile([P, count * P], U8, name=name + "_plane", align_bytes=64)
+            nc.vector.quantize_mx(
+                out=codes[:].bitcast(FP8X4), scales=plane[:], in_=grouped[:, first * P * PACK : (first + count) * P * PACK]
+            )
+            return [(codes[:, i * P : (i + 1) * P], plane[:, i * P : (i + 1) * P]) for i in range(count)]
 
-        def half_product(weights, t, h, acc):
-            codes, plane = weights[t // PAIR]
-            m_cols = slice((t % PAIR) * P, (t % PAIR + 1) * P)
+        def half_product(weights, h, acc):
+            codes, plane = weights
             nc.tensor.matmul_mx(
                 out=acc,
-                lhsT=codes[:, m_cols].bitcast(FP8X4),
-                lhsT_scale=plane[:, m_cols],
+                lhsT=codes.bitcast(FP8X4),
+                lhsT_scale=plane,
                 rhs=x_codes[h][:].bitcast(FP8X4),
                 rhs_scale=x_plane[:, h * HALF : (h + 1) * HALF],
                 start=True,
                 stop=True,
             )
 
-        def product(weights, t, dst):
+        def product(weights, dst):
             acc = psum.tile([P, S], F32, name="acc")
             for h in range(2):
-                half_product(weights, t, h, acc[:, h * HALF : (h + 1) * HALF])
+                half_product(weights, h, acc[:, h * HALF : (h + 1) * HALF])
             nc.scalar.copy(dst[:], acc[:])
 
-        def staging(pool, name, **where):
-            return pool.tile([P, PAIR * P * PACK], BF16, name=name, align_bytes=64, **where)
-
+        round_rows(nc.vector.tensor_copy, w1_raw[:, :, 0 : N // 2], 0, w1_bf)
+        round_rows(nc.scalar.copy, w1_raw[:, :, N // 2 : N], P // 2, w1_bf)
         nc.vector.tensor_copy(x_plane[:], scale_win[:].indirect(offs_t[:]))
-        g1 = [round_pair(nc.vector.tensor_copy, w1_raw, 0, staging(keep, "w1_lo")), round_pair(nc.scalar.copy, w1_raw, 1, staging(keep, "w1_hi"))]
-        q1 = [quantize_pair(g1[0], "w1_lo"), quantize_pair(g1[1], "w1_hi")]
+        q1 = quantize(w1_bf, 0, TILES, "w1")
         for h in range(2):
             nc.vector.tensor_copy(
                 x_codes[h][:],
                 word_win[:].bitcast(U32).indirect(offs_t[:, h * HALF // 16 : (h + 1) * HALF // 16]),
             )
-        nc.gpsimd.tensor_scalar(rest[:], share[:], -1.0, 1.0, MULT, ADD)
+        nc.scalar.activation(rest[:], share[:], COPY, bias=1.0, scale=-1.0)
 
         y = [keep.tile([P, S], F32, name=f"y{t}", align_bytes=64) for t in range(TILES)]
         e = [keep.tile([P, S], F32, name=f"e{t}", align_bytes=64) for t in range(TILES)]
-        kept = {t: keep.tile([P, V], F32, name=f"kept{t}", align_bytes=64) for t in (0, 2, 3)}
         drafted = [keep.tile([P, V], F32, name=f"drafted{t}", align_bytes=64) for t in range(TILES)]
         out_t = out.rearrange("(p t) s -> p t s", t=TILES)
+
+        for h in range(2):
+            acc = psum.tile([P, S], F32, name="acc")
+            half_product(q1[0], h, acc[:, 0:HALF])
+            nc.scalar.copy(y[0][:, h * HALF : (h + 1) * HALF], acc[:, 0:HALF])
+
+        round_rows(nc.vector.tensor_copy, w2_early[:], 0, w2_bf)
+        round_rows(nc.vector.tensor_copy, w2_late[:], P // 2, w2_bf)
+        kept = [late.tile([P, V], F32, name=f"kept{t}", align_bytes=64, offset=t * V * 4) for t in range(TILES)]
 
         def gather_y(t):
             nc.vector.tensor_tensor(kept[t][:], y[t][:].indirect(acc_t[:]), rest[:], MULT)
@@ -112,31 +124,19 @@ def tile_picked_specacc_none_p_kernel(tc, x_words, x_scales, w1, w2, sh, offs, a
             nc.vector.tensor_tensor(y[t][:].indirect(acc_t[:]), kept[t][:], drafted[t][:], ADD)
             nc.sync.dma_start(out_t[:, t, :], y[t][:])
 
-        for h in range(2):
-            acc = psum.tile([P, S], F32, name="acc")
-            half_product(q1, 0, h, acc[:, 0:HALF])
-            nc.scalar.copy(y[0][:, h * HALF : (h + 1) * HALF], acc[:, 0:HALF])
-        product(q1, 1, y[1])
-        product(q1, 2, y[2])
         gather_y(0)
-        g2_lo = round_pair(nc.vector.tensor_copy, w2_raw, 0, staging(reuse, "w2_lo", offset=0))
-        q2 = [quantize_pair(g2_lo, "w2_lo")]
-        kept[1] = reuse.tile([P, V], F32, name="kept1", align_bytes=64, offset=0)
-        gather_y(1)
-        product(q1, 3, y[3])
-        product(q2, 0, e[0])
-        product(q2, 1, e[1])
-        g2_hi = round_pair(nc.scalar.copy, w2_raw, 1, staging(reuse, "w2_hi", offset=V * 4))
-        gather_y(2)
-        gather_y(3)
+        q2 = quantize(w2_bf, 0, PAIR, "w2_lo") + quantize(w2_bf, PAIR, PAIR, "w2_hi")
+        for t in range(1, TILES):
+            product(q1[t], y[t])
+        for t in range(TILES):
+            product(q2[t], e[t])
+        for t in range(1, TILES):
+            gather_y(t)
         gather_e(0)
         gather_e(1)
         put(0)
-        q2.append(quantize_pair(g2_hi, "w2_hi"))
-        product(q2, 2, e[2])
-        product(q2, 3, e[3])
-        put(1)
         gather_e(2)
+        put(1)
         gather_e(3)
         put(2)
         put(3)

@@ -15,7 +15,6 @@ U8 = mybir.dt.uint8
 FP8X4 = mybir.dt.float8_e4m3fn_x4
 MULT = mybir.AluOpType.mult
 ADD = mybir.AluOpType.add
-COPY = mybir.ActivationFunctionType.Copy
 
 P = 128
 PACK = 4
@@ -28,7 +27,6 @@ def tile_picked_specacc_none_p_kernel(tc, x_words, x_scales, w1, w2, sh, offs, a
     nc = tc.nc
     with ExitStack() as ctx:
         keep = ctx.enter_context(tc.tile_pool(name="keep", bufs=1))
-        late = ctx.enter_context(tc.tile_pool(name="late", bufs=1))
         psum = ctx.enter_context(tc.psum_pool(name="psum", bufs=8))
 
         offs_t = keep.tile([P, S // 16], U16, name="offs_t")
@@ -37,13 +35,13 @@ def tile_picked_specacc_none_p_kernel(tc, x_words, x_scales, w1, w2, sh, offs, a
         word_win = keep.tile([P, T], I32, name="word_win", align_bytes=64)
         w1_raw = keep.tile([P, PACK, N], F32, name="w1_raw", align_bytes=64)
         w2_early = keep.tile([P, PACK, N // 2], F32, name="w2_early", align_bytes=64)
-        w2_late = late.tile([P, PACK, N // 2], F32, name="w2_late", align_bytes=64, offset=0)
+        w2_late = keep.tile([P, PACK, N // 2], F32, name="w2_late", align_bytes=64)
         share = keep.tile([P, V], F32, name="share", align_bytes=64)
         rest = keep.tile([P, V], F32, name="rest", align_bytes=64)
         x_codes = [keep.tile([P, HALF], U32, name=f"x_codes{h}", align_bytes=64) for h in range(2)]
         x_plane = keep.tile([P, S], U8, name="x_plane", align_bytes=64)
-        w1_bf = keep.tile([P, N * PACK], BF16, name="w1_bf", align_bytes=64)
-        w2_bf = keep.tile([P, N * PACK], BF16, name="w2_bf", align_bytes=64)
+        w1_bf = [keep.tile([P, PAIR * P * PACK], BF16, name=f"w1_bf{a}", align_bytes=64) for a in range(2)]
+        w2_bf = [keep.tile([P, PAIR * P * PACK], BF16, name=f"w2_bf{a}", align_bytes=64) for a in range(2)]
 
         nc.vector.memset(scale_win[:].bitcast(I32), 0)
         nc.sync.dma_start(offs_t[:], offs)
@@ -52,24 +50,22 @@ def tile_picked_specacc_none_p_kernel(tc, x_words, x_scales, w1, w2, sh, offs, a
         for r in range(4):
             nc.sync.dma_start(scale_win[r:P:32, :].bitcast(I32), scale_rows[r:16:4, :])
         nc.sync.dma_start(word_win[:], x_words[0].rearrange("p n t -> p (n t)").bitcast(I32))
-        nc.sync.dma_start(share[:], sh.rearrange("(p t) v -> p t v", t=TILES)[:, 0, :])
         w2_rows = w2.rearrange("(p j) n -> p j n", j=PACK)
         nc.sync.dma_start(w2_early[:], w2_rows[:, :, 0 : N // 2])
         nc.sync.dma_start(w2_late[:], w2_rows[:, :, N // 2 : N])
+        nc.sync.dma_start(share[:], sh.rearrange("(p t) v -> p t v", t=TILES)[:, 0, :])
         nc.sync.dma_start(acc_t[:], acc_l)
 
-        def round_rows(copy, raw, first, grouped):
+        def round_pair(copy, raw, first, pair, grouped):
             count = raw.shape[2] // TILES
-            dst = grouped[:].rearrange("p (t m j) -> p m j t", t=TILES, j=PACK)[:, first : first + count]
-            copy(dst, raw.rearrange("p j (m t) -> p m j t", t=TILES))
+            dst = grouped[pair][:].rearrange("p (t m j) -> p m j t", t=PAIR, j=PACK)[:, first : first + count]
+            copy(dst, raw[:].rearrange("p j (m t) -> p m j t", t=TILES)[:, :, :, PAIR * pair : PAIR * (pair + 1)])
 
-        def quantize(grouped, first, count, name):
-            codes = keep.tile([P, count * P], U32, name=name + "_codes", align_bytes=64)
-            plane = keep.tile([P, count * P], U8, name=name + "_plane", align_bytes=64)
-            nc.vector.quantize_mx(
-                out=codes[:].bitcast(FP8X4), scales=plane[:], in_=grouped[:, first * P * PACK : (first + count) * P * PACK]
-            )
-            return [(codes[:, i * P : (i + 1) * P], plane[:, i * P : (i + 1) * P]) for i in range(count)]
+        def quantize(grouped, name):
+            codes = keep.tile([P, PAIR * P], U32, name=name + "_codes", align_bytes=64)
+            plane = keep.tile([P, PAIR * P], U8, name=name + "_plane", align_bytes=64)
+            nc.vector.quantize_mx(out=codes[:].bitcast(FP8X4), scales=plane[:], in_=grouped[:])
+            return [(codes[:, i * P : (i + 1) * P], plane[:, i * P : (i + 1) * P]) for i in range(PAIR)]
 
         def half_product(weights, h, acc):
             codes, plane = weights
@@ -89,16 +85,15 @@ def tile_picked_specacc_none_p_kernel(tc, x_words, x_scales, w1, w2, sh, offs, a
                 half_product(weights, h, acc[:, h * HALF : (h + 1) * HALF])
             nc.scalar.copy(dst[:], acc[:])
 
-        round_rows(nc.vector.tensor_copy, w1_raw[:, :, 0 : N // 2], 0, w1_bf)
-        round_rows(nc.scalar.copy, w1_raw[:, :, N // 2 : N], P // 2, w1_bf)
+        round_pair(nc.vector.tensor_copy, w1_raw, 0, 0, w1_bf)
+        round_pair(nc.scalar.copy, w1_raw, 0, 1, w1_bf)
         nc.vector.tensor_copy(x_plane[:], scale_win[:].indirect(offs_t[:]))
-        q1 = quantize(w1_bf, 0, TILES, "w1")
+        q1 = quantize(w1_bf[0], "w1_lo") + quantize(w1_bf[1], "w1_hi")
         for h in range(2):
             nc.vector.tensor_copy(
                 x_codes[h][:],
                 word_win[:].bitcast(U32).indirect(offs_t[:, h * HALF // 16 : (h + 1) * HALF // 16]),
             )
-        nc.scalar.activation(rest[:], share[:], COPY, bias=1.0, scale=-1.0)
 
         y = [keep.tile([P, S], F32, name=f"y{t}", align_bytes=64) for t in range(TILES)]
         e = [keep.tile([P, S], F32, name=f"e{t}", align_bytes=64) for t in range(TILES)]
@@ -110,9 +105,10 @@ def tile_picked_specacc_none_p_kernel(tc, x_words, x_scales, w1, w2, sh, offs, a
             half_product(q1[0], h, acc[:, 0:HALF])
             nc.scalar.copy(y[0][:, h * HALF : (h + 1) * HALF], acc[:, 0:HALF])
 
-        round_rows(nc.vector.tensor_copy, w2_early[:], 0, w2_bf)
-        round_rows(nc.vector.tensor_copy, w2_late[:], P // 2, w2_bf)
-        kept = [late.tile([P, V], F32, name=f"kept{t}", align_bytes=64, offset=t * V * 4) for t in range(TILES)]
+        for raw, first in ((w2_early, 0), (w2_late, P // 2)):
+            for pair in range(2):
+                round_pair(nc.vector.tensor_copy, raw, first, pair, w2_bf)
+        kept = [keep.tile([P, V], F32, name=f"kept{t}", align_bytes=64) for t in range(TILES)]
 
         def gather_y(t):
             nc.vector.tensor_tensor(kept[t][:], y[t][:].indirect(acc_t[:]), rest[:], MULT)
@@ -124,13 +120,14 @@ def tile_picked_specacc_none_p_kernel(tc, x_words, x_scales, w1, w2, sh, offs, a
             nc.vector.tensor_tensor(y[t][:].indirect(acc_t[:]), kept[t][:], drafted[t][:], ADD)
             nc.sync.dma_start(out_t[:, t, :], y[t][:])
 
-        gather_y(0)
-        q2 = quantize(w2_bf, 0, PAIR, "w2_lo") + quantize(w2_bf, PAIR, PAIR, "w2_hi")
+        q2 = quantize(w2_bf[0], "w2_lo")
+        nc.vector.tensor_scalar(rest[:], share[:], -1.0, 1.0, MULT, ADD)
+        q2 = q2 + quantize(w2_bf[1], "w2_hi")
         for t in range(1, TILES):
             product(q1[t], y[t])
         for t in range(TILES):
             product(q2[t], e[t])
-        for t in range(1, TILES):
+        for t in range(TILES):
             gather_y(t)
         gather_e(0)
         gather_e(1)

@@ -27,6 +27,7 @@ def tile_picked_specacc_none_p_kernel(tc, x_words, x_scales, w1, w2, sh, offs, a
     nc = tc.nc
     with ExitStack() as ctx:
         keep = ctx.enter_context(tc.tile_pool(name="keep", bufs=1))
+        reuse = ctx.enter_context(tc.tile_pool(name="reuse", bufs=1))
         psum = ctx.enter_context(tc.psum_pool(name="psum", bufs=8))
 
         offs_t = keep.tile([P, S // 16], U16, name="offs_t")
@@ -36,24 +37,27 @@ def tile_picked_specacc_none_p_kernel(tc, x_words, x_scales, w1, w2, sh, offs, a
         w1_raw = keep.tile([P, PACK, N], F32, name="w1_raw", align_bytes=64)
         w2_early = keep.tile([P, PACK, N // 2], F32, name="w2_early", align_bytes=64)
         w2_late = keep.tile([P, PACK, N // 2], F32, name="w2_late", align_bytes=64)
-        share = keep.tile([P, V], F32, name="share", align_bytes=64)
+        picked = reuse.tile([P, S], U8, name="picked", align_bytes=64, offset=0)
         rest = keep.tile([P, V], F32, name="rest", align_bytes=64)
         x_codes = [keep.tile([P, HALF], U32, name=f"x_codes{h}", align_bytes=64) for h in range(2)]
         x_plane = keep.tile([P, S], U8, name="x_plane", align_bytes=64)
         w1_bf = [keep.tile([P, PAIR * P * PACK], BF16, name=f"w1_bf{a}", align_bytes=64) for a in range(2)]
         w2_bf = [keep.tile([P, PAIR * P * PACK], BF16, name=f"w2_bf{a}", align_bytes=64) for a in range(2)]
 
-        nc.vector.memset(scale_win[:].bitcast(I32), 0)
+        nc.scalar.dma_start(scale_win[16:32, :].bitcast(I32), x_scales[0].bitcast(I32))
+        warm = keep.tile([P, 16], F32, name="warm")
+        nc.gpsimd.memset(warm[:, 0:1], 0.0)
+        nc.scalar.copy(warm[:, 8:9], warm[:, 0:1])
+        nc.vector.memset(scale_win[0:16, :].bitcast(I32), 0)
+        nc.vector.memset(scale_win[32:64, :].bitcast(I32), 0)
+        nc.gpsimd.memset(scale_win[64:P, :].bitcast(I32), 0)
+        nc.gpsimd.memset(x_plane[:].bitcast(I32), 0)
         nc.sync.dma_start(offs_t[:], offs)
         nc.sync.dma_start(w1_raw[:], w1.rearrange("(p j) n -> p j n", j=PACK))
-        scale_rows = x_scales[0].bitcast(I32)
-        for r in range(4):
-            nc.sync.dma_start(scale_win[r:P:32, :].bitcast(I32), scale_rows[r:16:4, :])
         nc.sync.dma_start(word_win[:], x_words[0].rearrange("p n t -> p (n t)").bitcast(I32))
         w2_rows = w2.rearrange("(p j) n -> p j n", j=PACK)
         nc.sync.dma_start(w2_early[:], w2_rows[:, :, 0 : N // 2])
         nc.sync.dma_start(w2_late[:], w2_rows[:, :, N // 2 : N])
-        nc.sync.dma_start(share[:], sh.rearrange("(p t) v -> p t v", t=TILES)[:, 0, :])
         nc.sync.dma_start(acc_t[:], acc_l)
 
         def round_pair(copy, raw, first, pair, grouped):
@@ -85,9 +89,13 @@ def tile_picked_specacc_none_p_kernel(tc, x_words, x_scales, w1, w2, sh, offs, a
                 half_product(weights, h, acc[:, h * HALF : (h + 1) * HALF])
             nc.scalar.copy(dst[:], acc[:])
 
+        nc.vector.tensor_copy(picked[:], scale_win[:].indirect(offs_t[:]))
+        for r in range(4):
+            nc.scalar.dma_start(x_plane[r:P:32, :].bitcast(I32), picked[16 + r : 32 : 4, :].bitcast(I32))
+        share = reuse.tile([P, V], F32, name="share", align_bytes=64, offset=0)
+        nc.sync.dma_start(share[:], sh.rearrange("(p t) v -> p t v", t=TILES)[:, 0, :])
         round_pair(nc.vector.tensor_copy, w1_raw, 0, 0, w1_bf)
         round_pair(nc.scalar.copy, w1_raw, 0, 1, w1_bf)
-        nc.vector.tensor_copy(x_plane[:], scale_win[:].indirect(offs_t[:]))
         q1 = quantize(w1_bf[0], "w1_lo") + quantize(w1_bf[1], "w1_hi")
         for h in range(2):
             nc.vector.tensor_copy(

@@ -1,6 +1,7 @@
 from contextlib import ExitStack
 
 import concourse.mybir as mybir
+from concourse.masks import make_identity
 
 K, T, S, V, N = 512, 2048, 512, 256, 512
 FLOPS = 2 * 2 * K * N * S
@@ -32,33 +33,32 @@ def tile_picked_specacc_none_p_kernel(tc, x_words, x_scales, w1, w2, sh, offs, a
 
         offs_t = keep.tile([P, S // 16], U16, name="offs_t")
         acc_t = keep.tile([P, V // 16], U16, name="acc_t")
-        scale_win = keep.tile([P, T], U8, name="scale_win", align_bytes=64)
         word_win = keep.tile([P, T], I32, name="word_win", align_bytes=64)
         w1_raw = keep.tile([P, PACK, N], F32, name="w1_raw", align_bytes=64)
-        w2_early = keep.tile([P, PACK, N // 2], F32, name="w2_early", align_bytes=64)
-        w2_late = keep.tile([P, PACK, N // 2], F32, name="w2_late", align_bytes=64)
-        picked = reuse.tile([P, S], U8, name="picked", align_bytes=64, offset=0)
+        picked = keep.tile([P, S], U8, name="picked", align_bytes=64)
         rest = keep.tile([P, V], F32, name="rest", align_bytes=64)
-        x_codes = [keep.tile([P, HALF], U32, name=f"x_codes{h}", align_bytes=64) for h in range(2)]
+        x_codes = keep.tile([P, S], U32, name="x_codes", align_bytes=64)
         x_plane = keep.tile([P, S], U8, name="x_plane", align_bytes=64)
         w1_bf = [keep.tile([P, PAIR * P * PACK], BF16, name=f"w1_bf{a}", align_bytes=64) for a in range(2)]
         w2_bf = [keep.tile([P, PAIR * P * PACK], BF16, name=f"w2_bf{a}", align_bytes=64) for a in range(2)]
+        scale_win = reuse.tile([P, T], U8, name="scale_win", align_bytes=64, offset=3584)
 
-        nc.scalar.dma_start(scale_win[16:32, :].bitcast(I32), x_scales[0].bitcast(I32))
-        warm = keep.tile([P, 16], F32, name="warm")
-        nc.gpsimd.memset(warm[:, 0:1], 0.0)
-        nc.scalar.copy(warm[:, 8:9], warm[:, 0:1])
+        nc.sync.dma_start(scale_win[16:32, :].bitcast(I32), x_scales[0].bitcast(I32))
         nc.vector.memset(scale_win[0:16, :].bitcast(I32), 0)
         nc.vector.memset(scale_win[32:64, :].bitcast(I32), 0)
-        nc.gpsimd.memset(scale_win[64:P, :].bitcast(I32), 0)
-        nc.gpsimd.memset(x_plane[:].bitcast(I32), 0)
+        nc.vector.memset(scale_win[64:P, :].bitcast(I32), 0)
+        nc.vector.memset(x_plane[:].bitcast(I32), 0)
+        share_rows = keep.tile([P, V], F32, name="share_rows", align_bytes=64)
+        ident = keep.tile([P, P], F32, name="ident", align_bytes=64)
+        nc.gpsimd.memset(share_rows[0:24, :], 0.0)
+        nc.gpsimd.memset(share_rows[32:64, :], 0.0)
+        nc.gpsimd.memset(share_rows[64:P, :], 0.0)
+        make_identity(nc, ident[:])
         nc.sync.dma_start(offs_t[:], offs)
+        nc.sync.dma_start(share_rows[24:32, :], sh.rearrange("(g r) v -> g r v", r=64)[:, 0, :])
         nc.sync.dma_start(w1_raw[:], w1.rearrange("(p j) n -> p j n", j=PACK))
-        nc.sync.dma_start(word_win[:], x_words[0].rearrange("p n t -> p (n t)").bitcast(I32))
-        w2_rows = w2.rearrange("(p j) n -> p j n", j=PACK)
-        nc.sync.dma_start(w2_early[:], w2_rows[:, :, 0 : N // 2])
-        nc.sync.dma_start(w2_late[:], w2_rows[:, :, N // 2 : N])
         nc.sync.dma_start(acc_t[:], acc_l)
+        nc.sync.dma_start(word_win[:], x_words[0].rearrange("p n t -> p (n t)").bitcast(I32))
 
         def round_pair(copy, raw, first, pair, grouped):
             count = raw.shape[2] // TILES
@@ -71,35 +71,48 @@ def tile_picked_specacc_none_p_kernel(tc, x_words, x_scales, w1, w2, sh, offs, a
             nc.vector.quantize_mx(out=codes[:].bitcast(FP8X4), scales=plane[:], in_=grouped[:])
             return [(codes[:, i * P : (i + 1) * P], plane[:, i * P : (i + 1) * P]) for i in range(PAIR)]
 
-        def half_product(weights, h, acc):
+        def product(weights, dst, cols):
             codes, plane = weights
+            acc = psum.tile([P, S], F32, name="acc")
             nc.tensor.matmul_mx(
-                out=acc,
+                out=acc[:, cols],
                 lhsT=codes.bitcast(FP8X4),
                 lhsT_scale=plane,
-                rhs=x_codes[h][:].bitcast(FP8X4),
-                rhs_scale=x_plane[:, h * HALF : (h + 1) * HALF],
+                rhs=x_codes[:, cols].bitcast(FP8X4),
+                rhs_scale=x_plane[:, cols],
                 start=True,
                 stop=True,
             )
-
-        def product(weights, dst):
-            acc = psum.tile([P, S], F32, name="acc")
-            for h in range(2):
-                half_product(weights, h, acc[:, h * HALF : (h + 1) * HALF])
-            nc.scalar.copy(dst[:], acc[:])
+            nc.scalar.copy(dst[:, cols], acc[:, cols])
 
         nc.vector.tensor_copy(picked[:], scale_win[:].indirect(offs_t[:]))
         for r in range(4):
-            nc.scalar.dma_start(x_plane[r:P:32, :].bitcast(I32), picked[16 + r : 32 : 4, :].bitcast(I32))
-        share = reuse.tile([P, V], F32, name="share", align_bytes=64, offset=0)
-        nc.sync.dma_start(share[:], sh.rearrange("(p t) v -> p t v", t=TILES)[:, 0, :])
+            nc.sync.dma_start(x_plane[r:P:32, :].bitcast(I32), picked[16 + r : 32 : 4, :].bitcast(I32))
+        w2_early = reuse.tile([P, PACK, N // 2], F32, name="w2_early", align_bytes=64, offset=0)
+        w2_late = reuse.tile([P, PACK, N // 2], F32, name="w2_late", align_bytes=64, offset=4096)
+        w2_rows = w2.rearrange("(p j) n -> p j n", j=PACK)
+        nc.sync.dma_start(w2_early[:], w2_rows[:, :, 0 : N // 2])
+        nc.sync.dma_start(w2_late[:], w2_rows[:, :, N // 2 : N])
+        spread = keep.tile([P, 2, P], F32, name="spread", align_bytes=64)
+        share = keep.tile([P, V], F32, name="share", align_bytes=64)
+        turned = psum.tile([P, S], F32, name="acc")
+        for c in range(2):
+            nc.tensor.transpose(turned[:, c * P : (c + 1) * P], share_rows[:, c * P : (c + 1) * P], ident[:])
+        nc.scalar.copy(
+            spread[:].rearrange("p c (g r) -> p c g r", r=16),
+            turned[:, 0:V].rearrange("p (c k o) -> p c k o", c=2, o=1)[:, :, 24:32, :].to_broadcast([P, 2, 8, 16]),
+        )
+        back = psum.tile([P, S], F32, name="acc")
+        for c in range(2):
+            nc.tensor.transpose(back[:, c * P : (c + 1) * P], spread[:, c, :], ident[:])
+        nc.scalar.copy(share[:], back[:, 0:V])
+        nc.scalar.activation(rest[:], back[:, 0:V], mybir.ActivationFunctionType.Copy, bias=1.0, scale=-1.0)
         round_pair(nc.vector.tensor_copy, w1_raw, 0, 0, w1_bf)
         round_pair(nc.scalar.copy, w1_raw, 0, 1, w1_bf)
         q1 = quantize(w1_bf[0], "w1_lo") + quantize(w1_bf[1], "w1_hi")
         for h in range(2):
             nc.vector.tensor_copy(
-                x_codes[h][:],
+                x_codes[:, h * HALF : (h + 1) * HALF],
                 word_win[:].bitcast(U32).indirect(offs_t[:, h * HALF // 16 : (h + 1) * HALF // 16]),
             )
 
@@ -109,14 +122,9 @@ def tile_picked_specacc_none_p_kernel(tc, x_words, x_scales, w1, w2, sh, offs, a
         out_t = out.rearrange("(p t) s -> p t s", t=TILES)
 
         for h in range(2):
-            acc = psum.tile([P, S], F32, name="acc")
-            half_product(q1[0], h, acc[:, 0:HALF])
-            nc.scalar.copy(y[0][:, h * HALF : (h + 1) * HALF], acc[:, 0:HALF])
-
-        for raw, first in ((w2_early, 0), (w2_late, P // 2)):
-            for pair in range(2):
-                round_pair(nc.vector.tensor_copy, raw, first, pair, w2_bf)
-        kept = [keep.tile([P, V], F32, name=f"kept{t}", align_bytes=64) for t in range(TILES)]
+            product(q1[0], y[0], slice(h * HALF, (h + 1) * HALF))
+        for t in range(1, TILES):
+            product(q1[t], y[t], slice(0, S))
 
         def gather_y(t):
             nc.vector.tensor_tensor(kept[t][:], y[t][:].indirect(acc_t[:]), rest[:], MULT)
@@ -128,13 +136,16 @@ def tile_picked_specacc_none_p_kernel(tc, x_words, x_scales, w1, w2, sh, offs, a
             nc.vector.tensor_tensor(y[t][:].indirect(acc_t[:]), kept[t][:], drafted[t][:], ADD)
             nc.sync.dma_start(out_t[:, t, :], y[t][:])
 
-        q2 = quantize(w2_bf[0], "w2_lo")
-        nc.vector.tensor_scalar(rest[:], share[:], -1.0, 1.0, MULT, ADD)
-        q2 = q2 + quantize(w2_bf[1], "w2_hi")
-        for t in range(1, TILES):
-            product(q1[t], y[t])
+        for pair in range(2):
+            round_pair(nc.vector.tensor_copy, w2_early, 0, pair, w2_bf)
+        for pair in range(2):
+            round_pair(nc.vector.tensor_copy, w2_late, P // 2, pair, w2_bf)
+        q2 = quantize(w2_bf[0], "w2_lo") + quantize(w2_bf[1], "w2_hi")
+        kept = [
+            reuse.tile([P, V], F32, name=f"kept{t}", align_bytes=64, offset=4096 + 1024 * t) for t in range(TILES)
+        ]
         for t in range(TILES):
-            product(q2[t], e[t])
+            product(q2[t], e[t], slice(0, S))
         for t in range(TILES):
             gather_y(t)
         gather_e(0)

@@ -43,19 +43,19 @@ def tile_picked_specacc_none_p_kernel(tc, x_words, x_scales, w1, w2, sh, offs, a
         w2_bf = [keep.tile([P, PAIR * P * PACK], BF16, name=f"w2_bf{a}", align_bytes=64) for a in range(2)]
         scale_win = reuse.tile([P, T], U8, name="scale_win", align_bytes=64, offset=3584)
 
-        nc.sync.dma_start(scale_win[16:32, :].bitcast(I32), x_scales[0].bitcast(I32))
+        nc.scalar.dma_start(scale_win[16:32, :].bitcast(I32), x_scales[0].bitcast(I32))
         nc.vector.memset(scale_win[0:16, :].bitcast(I32), 0)
         nc.vector.memset(scale_win[32:64, :].bitcast(I32), 0)
         nc.vector.memset(scale_win[64:P, :].bitcast(I32), 0)
         nc.vector.memset(x_plane[:].bitcast(I32), 0)
         share_rows = keep.tile([P, V], F32, name="share_rows", align_bytes=64)
         ident = keep.tile([P, P], F32, name="ident", align_bytes=64)
-        nc.gpsimd.memset(share_rows[0:24, :], 0.0)
-        nc.gpsimd.memset(share_rows[32:64, :], 0.0)
-        nc.gpsimd.memset(share_rows[64:P, :], 0.0)
+        nc.gpsimd.memset(share_rows[0:64, :], 0.0)
+        nc.gpsimd.memset(share_rows[64:88, :], 0.0)
+        nc.gpsimd.memset(share_rows[96:P, :], 0.0)
         make_identity(nc, ident[:])
         nc.sync.dma_start(offs_t[:], offs)
-        nc.sync.dma_start(share_rows[24:32, :], sh.rearrange("(g r) v -> g r v", r=64)[:, 0, :])
+        nc.scalar.dma_start(share_rows[88:96, :], sh.rearrange("(g r) v -> g r v", r=64)[:, 0, :])
         nc.sync.dma_start(w1_raw[:], w1.rearrange("(p j) n -> p j n", j=PACK))
         nc.sync.dma_start(acc_t[:], acc_l)
         nc.sync.dma_start(word_win[:], x_words[0].rearrange("p n t -> p (n t)").bitcast(I32))
@@ -100,7 +100,7 @@ def tile_picked_specacc_none_p_kernel(tc, x_words, x_scales, w1, w2, sh, offs, a
             nc.tensor.transpose(turned[:, c * P : (c + 1) * P], share_rows[:, c * P : (c + 1) * P], ident[:])
         nc.scalar.copy(
             spread[:].rearrange("p c (g r) -> p c g r", r=16),
-            turned[:, 0:V].rearrange("p (c k o) -> p c k o", c=2, o=1)[:, :, 24:32, :].to_broadcast([P, 2, 8, 16]),
+            turned[:, 0:V].rearrange("p (c k o) -> p c k o", c=2, o=1)[:, :, 88:96, :].to_broadcast([P, 2, 8, 16]),
         )
         back = psum.tile([P, S], F32, name="acc")
         for c in range(2):
@@ -110,20 +110,14 @@ def tile_picked_specacc_none_p_kernel(tc, x_words, x_scales, w1, w2, sh, offs, a
         round_pair(nc.vector.tensor_copy, w1_raw, 0, 0, w1_bf)
         round_pair(nc.scalar.copy, w1_raw, 0, 1, w1_bf)
         q1 = quantize(w1_bf[0], "w1_lo") + quantize(w1_bf[1], "w1_hi")
-        for h in range(2):
-            nc.vector.tensor_copy(
-                x_codes[:, h * HALF : (h + 1) * HALF],
-                word_win[:].bitcast(U32).indirect(offs_t[:, h * HALF // 16 : (h + 1) * HALF // 16]),
-            )
+        nc.vector.tensor_copy(x_codes[:], word_win[:].bitcast(U32).indirect(offs_t[:]))
 
         y = [keep.tile([P, S], F32, name=f"y{t}", align_bytes=64) for t in range(TILES)]
         e = [keep.tile([P, S], F32, name=f"e{t}", align_bytes=64) for t in range(TILES)]
         drafted = [keep.tile([P, V], F32, name=f"drafted{t}", align_bytes=64) for t in range(TILES)]
         out_t = out.rearrange("(p t) s -> p t s", t=TILES)
 
-        for h in range(2):
-            product(q1[0], y[0], slice(h * HALF, (h + 1) * HALF))
-        for t in range(1, TILES):
+        for t in range(TILES):
             product(q1[t], y[t], slice(0, S))
 
         def gather_y(t):
@@ -138,9 +132,25 @@ def tile_picked_specacc_none_p_kernel(tc, x_words, x_scales, w1, w2, sh, offs, a
 
         for pair in range(2):
             round_pair(nc.vector.tensor_copy, w2_early, 0, pair, w2_bf)
+        w2_codes = keep.tile([P, TILES, P], U32, name="w2_codes", align_bytes=64)
+        w2_plane = keep.tile([P, TILES, P], U8, name="w2_plane", align_bytes=64)
+
+        def quantize_half(t, half):
+            cols = slice(half * P // 2, (half + 1) * P // 2)
+            first = ((t % PAIR) * P + cols.start) * PACK
+            nc.vector.quantize_mx(
+                out=w2_codes[:, t, cols].bitcast(FP8X4),
+                scales=w2_plane[:, t, cols],
+                in_=w2_bf[t // PAIR][:, first : first + P // 2 * PACK],
+            )
+
+        for t in range(TILES):
+            quantize_half(t, 0)
         for pair in range(2):
             round_pair(nc.vector.tensor_copy, w2_late, P // 2, pair, w2_bf)
-        q2 = quantize(w2_bf[0], "w2_lo") + quantize(w2_bf[1], "w2_hi")
+        for t in range(TILES):
+            quantize_half(t, 1)
+        q2 = [(w2_codes[:, t, :], w2_plane[:, t, :]) for t in range(TILES)]
         kept = [
             reuse.tile([P, V], F32, name=f"kept{t}", align_bytes=64, offset=4096 + 1024 * t) for t in range(TILES)
         ]

@@ -61,9 +61,10 @@ def tile_picked_specacc_none_p_kernel(tc, x_words, x_scales, w1, w2, sh, offs, a
         nc.sync.dma_start(word_win[:], x_words[0].rearrange("p n t -> p (n t)").bitcast(I32))
 
         def round_pair(copy, raw, first, pair, grouped):
-            count = raw.shape[2] // TILES
-            dst = grouped[pair][:].rearrange("p (t m j) -> p m j t", t=PAIR, j=PACK)[:, first : first + count]
-            copy(dst, raw[:].rearrange("p j (m t) -> p m j t", t=TILES)[:, :, :, PAIR * pair : PAIR * (pair + 1)])
+            count = raw.shape[2] // (2 * TILES)
+            dst = grouped[pair][:].rearrange("p (t a i j) -> p t a j i", t=PAIR, i=2, j=PACK)
+            src = raw[:].rearrange("p j (a t i) -> p t a j i", t=TILES, i=2)
+            copy(dst[:, :, first // 2 : first // 2 + count], src[:, PAIR * pair : PAIR * (pair + 1)])
 
         def quantize(grouped, name):
             codes = keep.tile([P, PAIR * P], U32, name=name + "_codes", align_bytes=64)
@@ -115,7 +116,7 @@ def tile_picked_specacc_none_p_kernel(tc, x_words, x_scales, w1, w2, sh, offs, a
         y = [keep.tile([P, S], F32, name=f"y{t}", align_bytes=64) for t in range(TILES)]
         e = [keep.tile([P, S], F32, name=f"e{t}", align_bytes=64) for t in range(TILES)]
         drafted = [keep.tile([P, V], F32, name=f"drafted{t}", align_bytes=64) for t in range(TILES)]
-        out_t = out.rearrange("(p t) s -> p t s", t=TILES)
+        out_t = out.rearrange("(a t i) s -> t a i s", t=TILES, i=2)
 
         for t in range(TILES):
             product(q1[t], y[t], slice(0, S))
@@ -128,7 +129,7 @@ def tile_picked_specacc_none_p_kernel(tc, x_words, x_scales, w1, w2, sh, offs, a
 
         def put(t):
             nc.vector.tensor_tensor(y[t][:].indirect(acc_t[:]), kept[t][:], drafted[t][:], ADD)
-            nc.sync.dma_start(out_t[:, t, :], y[t][:])
+            nc.sync.dma_start(out_t[t], y[t][:])
 
         for pair in range(2):
             round_pair(nc.vector.tensor_copy, w2_early, 0, pair, w2_bf)

@@ -16,12 +16,16 @@ U8 = mybir.dt.uint8
 FP8X4 = mybir.dt.float8_e4m3fn_x4
 MULT = mybir.AluOpType.mult
 ADD = mybir.AluOpType.add
+SUB = mybir.AluOpType.subtract
+COPY = mybir.ActivationFunctionType.Copy
 
 P = 128
 PACK = 4
 TILES = N // P
 PAIR = 2
 HALF = S // 2
+WHOLE = slice(0, S)
+HALVES = (slice(0, HALF), slice(HALF, S))
 
 
 def tile_picked_specacc_none_p_kernel(tc, x_words, x_scales, w1, w2, sh, offs, acc_l, out):
@@ -36,7 +40,6 @@ def tile_picked_specacc_none_p_kernel(tc, x_words, x_scales, w1, w2, sh, offs, a
         word_win = keep.tile([P, T], I32, name="word_win", align_bytes=64)
         w1_raw = keep.tile([P, PACK, N], F32, name="w1_raw", align_bytes=64)
         picked = keep.tile([P, S], U8, name="picked", align_bytes=64)
-        rest = keep.tile([P, V], F32, name="rest", align_bytes=64)
         x_codes = keep.tile([P, S], U32, name="x_codes", align_bytes=64)
         x_plane = keep.tile([P, S], U8, name="x_plane", align_bytes=64)
         w1_bf = [keep.tile([P, PAIR * P * PACK], BF16, name=f"w1_bf{a}", align_bytes=64) for a in range(2)]
@@ -60,11 +63,12 @@ def tile_picked_specacc_none_p_kernel(tc, x_words, x_scales, w1, w2, sh, offs, a
         nc.sync.dma_start(acc_t[:], acc_l)
         nc.sync.dma_start(word_win[:], x_words[0].rearrange("p n t -> p (n t)").bitcast(I32))
 
-        def round_pair(copy, raw, first, pair, grouped):
+        def round_tiles(copy, raw, first, tiles, grouped):
             count = raw.shape[2] // (2 * TILES)
+            pair, lo = divmod(tiles.start, PAIR)
             dst = grouped[pair][:].rearrange("p (t a i j) -> p t a j i", t=PAIR, i=2, j=PACK)
             src = raw[:].rearrange("p j (a t i) -> p t a j i", t=TILES, i=2)
-            copy(dst[:, :, first // 2 : first // 2 + count], src[:, PAIR * pair : PAIR * (pair + 1)])
+            copy(dst[:, lo : lo + tiles.stop - tiles.start, first // 2 : first // 2 + count], src[:, tiles])
 
         def quantize(grouped, name):
             codes = keep.tile([P, PAIR * P], U32, name=name + "_codes", align_bytes=64)
@@ -72,19 +76,26 @@ def tile_picked_specacc_none_p_kernel(tc, x_words, x_scales, w1, w2, sh, offs, a
             nc.vector.quantize_mx(out=codes[:].bitcast(FP8X4), scales=plane[:], in_=grouped[:])
             return [(codes[:, i * P : (i + 1) * P], plane[:, i * P : (i + 1) * P]) for i in range(PAIR)]
 
-        def product(weights, dst, cols):
+        def product(weights, parts):
             codes, plane = weights
-            acc = psum.tile([P, S], F32, name="acc")
-            nc.tensor.matmul_mx(
-                out=acc[:, cols],
-                lhsT=codes.bitcast(FP8X4),
-                lhsT_scale=plane,
-                rhs=x_codes[:, cols].bitcast(FP8X4),
-                rhs_scale=x_plane[:, cols],
-                start=True,
-                stop=True,
-            )
-            nc.scalar.copy(dst[:, cols], acc[:, cols])
+            banks = []
+            for cols in parts:
+                acc = psum.tile([P, S], F32, name="acc")
+                nc.tensor.matmul_mx(
+                    out=acc[:, cols],
+                    lhsT=codes.bitcast(FP8X4),
+                    lhsT_scale=plane,
+                    rhs=x_codes[:, cols].bitcast(FP8X4),
+                    rhs_scale=x_plane[:, cols],
+                    start=True,
+                    stop=True,
+                )
+                banks.append((acc, cols))
+            return banks
+
+        def empty(banks, dst, copy=nc.scalar.copy):
+            for acc, cols in banks:
+                copy(dst[:, cols], acc[:, cols])
 
         nc.vector.tensor_copy(picked[:], scale_win[:].indirect(offs_t[:]))
         for r in range(4):
@@ -95,7 +106,7 @@ def tile_picked_specacc_none_p_kernel(tc, x_words, x_scales, w1, w2, sh, offs, a
         nc.sync.dma_start(w2_early[:], w2_rows[:, :, 0 : N // 2])
         nc.sync.dma_start(w2_late[:], w2_rows[:, :, N // 2 : N])
         spread = keep.tile([P, 2, P], F32, name="spread", align_bytes=64)
-        share = keep.tile([P, V], F32, name="share", align_bytes=64)
+        mix = keep.tile([P, 2, V], F32, name="mix", align_bytes=64)
         turned = psum.tile([P, S], F32, name="acc")
         for c in range(2):
             nc.tensor.transpose(turned[:, c * P : (c + 1) * P], share_rows[:, c * P : (c + 1) * P], ident[:])
@@ -106,64 +117,71 @@ def tile_picked_specacc_none_p_kernel(tc, x_words, x_scales, w1, w2, sh, offs, a
         back = psum.tile([P, S], F32, name="acc")
         for c in range(2):
             nc.tensor.transpose(back[:, c * P : (c + 1) * P], spread[:, c, :], ident[:])
-        nc.scalar.copy(share[:], back[:, 0:V])
-        nc.scalar.activation(rest[:], back[:, 0:V], mybir.ActivationFunctionType.Copy, bias=1.0, scale=-1.0)
-        round_pair(nc.vector.tensor_copy, w1_raw, 0, 0, w1_bf)
-        round_pair(nc.scalar.copy, w1_raw, 0, 1, w1_bf)
+        nc.scalar.copy(mix[:, 1, :], back[:, 0:V])
+        nc.scalar.activation(mix[:, 0, :], back[:, 0:V], COPY, bias=1.0, scale=-1.0)
+        round_tiles(nc.vector.tensor_copy, w1_raw, 0, slice(0, 2), w1_bf)
+        round_tiles(nc.scalar.copy, w1_raw, 0, slice(2, 4), w1_bf)
         q1 = quantize(w1_bf[0], "w1_lo") + quantize(w1_bf[1], "w1_hi")
-        nc.vector.tensor_copy(x_codes[:], word_win[:].bitcast(U32).indirect(offs_t[:]))
+        for cols in HALVES:
+            nc.vector.tensor_copy(
+                x_codes[:, cols], word_win[:].bitcast(U32).indirect(offs_t[:, cols.start // 16 : cols.stop // 16])
+            )
 
-        y = [keep.tile([P, S], F32, name=f"y{t}", align_bytes=64) for t in range(TILES)]
+        y = [keep.tile([P, S], F32, name=f"y{t}", align_bytes=64) for t in range(2)]
         e = [keep.tile([P, S], F32, name=f"e{t}", align_bytes=64) for t in range(TILES)]
-        drafted = [keep.tile([P, V], F32, name=f"drafted{t}", align_bytes=64) for t in range(TILES)]
+        found = [keep.tile([P, 2, V], F32, name=f"found{t}", align_bytes=64) for t in range(TILES)]
         out_t = out.rearrange("(a t i) s -> t a i s", t=TILES, i=2)
 
-        for t in range(TILES):
-            product(q1[t], y[t], slice(0, S))
+        def fetch(t, side, rows):
+            nc.scalar.activation(found[t][:, side, :], rows[t][:].indirect(acc_t[:]), COPY)
 
-        def gather_y(t):
-            nc.vector.tensor_tensor(kept[t][:], y[t][:].indirect(acc_t[:]), rest[:], MULT)
+        y_banks = [product(q1[t], HALVES if t == 0 else [WHOLE]) for t in range(TILES)]
+        for t in range(2):
+            empty(y_banks[t], y[t])
+        for t in range(2):
+            fetch(t, 0, y)
 
-        def gather_e(t):
-            nc.vector.tensor_tensor(drafted[t][:], e[t][:].indirect(acc_t[:]), share[:], MULT)
-
-        def put(t):
-            nc.vector.tensor_tensor(y[t][:].indirect(acc_t[:]), kept[t][:], drafted[t][:], ADD)
-            nc.sync.dma_start(out_t[t], y[t][:])
-
-        for pair in range(2):
-            round_pair(nc.vector.tensor_copy, w2_early, 0, pair, w2_bf)
-        w2_codes = keep.tile([P, TILES, P], U32, name="w2_codes", align_bytes=64)
+        w2_codes = [
+            reuse.tile([P, P], U32, name=f"w2_codes{t}", align_bytes=64, offset=at)
+            for t, at in enumerate((12288, 13824, 12800, 13312))
+        ]
         w2_plane = keep.tile([P, TILES, P], U8, name="w2_plane", align_bytes=64)
 
         def quantize_half(t, half):
             cols = slice(half * P // 2, (half + 1) * P // 2)
             first = ((t % PAIR) * P + cols.start) * PACK
             nc.vector.quantize_mx(
-                out=w2_codes[:, t, cols].bitcast(FP8X4),
+                out=w2_codes[t][:, cols].bitcast(FP8X4),
                 scales=w2_plane[:, t, cols],
                 in_=w2_bf[t // PAIR][:, first : first + P // 2 * PACK],
             )
 
-        for t in range(TILES):
-            quantize_half(t, 0)
-        for pair in range(2):
-            round_pair(nc.vector.tensor_copy, w2_late, P // 2, pair, w2_bf)
-        for t in range(TILES):
-            quantize_half(t, 1)
-        q2 = [(w2_codes[:, t, :], w2_plane[:, t, :]) for t in range(TILES)]
-        kept = [
-            reuse.tile([P, V], F32, name=f"kept{t}", align_bytes=64, offset=4096 + 1024 * t) for t in range(TILES)
-        ]
-        for t in range(TILES):
-            product(q2[t], e[t], slice(0, S))
-        for t in range(TILES):
-            gather_y(t)
-        gather_e(0)
-        gather_e(1)
-        put(0)
-        gather_e(2)
-        put(1)
-        gather_e(3)
-        put(2)
-        put(3)
+        for half, raw in enumerate((w2_early, w2_late)):
+            for pair in range(2):
+                round_tiles(nc.vector.tensor_copy, raw, half * P // 2, slice(2 * pair, 2 * pair + 2), w2_bf)
+            for t in range(TILES):
+                quantize_half(t, half)
+        q2 = [(w2_codes[t][:], w2_plane[:, t, :]) for t in range(TILES)]
+        e_banks = [product(q2[t], [WHOLE]) for t in range(TILES)]
+        y += [reuse.tile([P, S], F32, name=f"y{t}", align_bytes=64, offset=4096 + 2048 * t) for t in range(2, TILES)]
+        pulls = [keep.tile([P, V], F32, name=f"pull{t}", align_bytes=64) for t in range(2)]
+        terms = {t: keep.tile([P, 2, V], F32, name=f"terms{t}", align_bytes=64) for t in range(2, TILES)}
+
+        def put(t, first, second):
+            nc.vector.tensor_tensor(y[t][:].indirect(acc_t[:]), first, second, ADD)
+            nc.sync.dma_start(out_t[t], y[t][:])
+
+        for t in range(2):
+            nc.vector.tensor_tensor(e[t][:], e_banks[t][0][0][:], y[t][:], SUB)
+        for t in range(2):
+            nc.vector.tensor_tensor(pulls[t][:], e[t][:].indirect(acc_t[:]), mix[:, 1, :], MULT)
+        for t in range(2, TILES):
+            empty(y_banks[t], y[t])
+            empty(e_banks[t], e[t])
+            fetch(t, 0, y)
+            fetch(t, 1, e)
+        for t in range(2):
+            put(t, found[t][:, 0, :], pulls[t][:])
+            nc.vector.tensor_tensor(terms[t + 2][:], found[t + 2][:], mix[:], MULT)
+        for t in range(2, TILES):
+            put(t, terms[t][:, 0, :], terms[t][:, 1, :])

@@ -33,7 +33,7 @@ def tile_picked_specacc_none_p_kernel(tc, x_words, x_scales, w1, w2, sh, offs, a
     with ExitStack() as ctx:
         keep = ctx.enter_context(tc.tile_pool(name="keep", bufs=1))
         reuse = ctx.enter_context(tc.tile_pool(name="reuse", bufs=1))
-        psum = ctx.enter_context(tc.psum_pool(name="psum", bufs=8))
+        psum = ctx.enter_context(tc.psum_pool(name="psum", bufs=1))
 
         offs_t = keep.tile([P, S // 16], U16, name="offs_t")
         acc_t = keep.tile([P, V // 16], U16, name="acc_t")
@@ -68,7 +68,10 @@ def tile_picked_specacc_none_p_kernel(tc, x_words, x_scales, w1, w2, sh, offs, a
             pair, lo = divmod(tiles.start, PAIR)
             dst = grouped[pair][:].rearrange("p (t a i j) -> p t a j i", t=PAIR, i=2, j=PACK)
             src = raw[:].rearrange("p j (a t i) -> p t a j i", t=TILES, i=2)
-            copy(dst[:, lo : lo + tiles.stop - tiles.start, first // 2 : first // 2 + count], src[:, tiles])
+            if tiles.stop - tiles.start == 1:
+                copy(dst[:, lo, first // 2 : first // 2 + count], src[:, tiles.start])
+            else:
+                copy(dst[:, :, first // 2 : first // 2 + count], src[:, tiles])
 
         def quantize(grouped, name):
             codes = keep.tile([P, PAIR * P], U32, name=name + "_codes", align_bytes=64)
@@ -76,26 +79,24 @@ def tile_picked_specacc_none_p_kernel(tc, x_words, x_scales, w1, w2, sh, offs, a
             nc.vector.quantize_mx(out=codes[:].bitcast(FP8X4), scales=plane[:], in_=grouped[:])
             return [(codes[:, i * P : (i + 1) * P], plane[:, i * P : (i + 1) * P]) for i in range(PAIR)]
 
-        def product(weights, parts):
-            codes, plane = weights
-            banks = []
-            for cols in parts:
-                acc = psum.tile([P, S], F32, name="acc")
-                nc.tensor.matmul_mx(
-                    out=acc[:, cols],
-                    lhsT=codes.bitcast(FP8X4),
-                    lhsT_scale=plane,
-                    rhs=x_codes[:, cols].bitcast(FP8X4),
-                    rhs_scale=x_plane[:, cols],
-                    start=True,
-                    stop=True,
-                )
-                banks.append((acc, cols))
-            return banks
+        def bank(number):
+            return psum.tile([P, S], F32, name=f"bank{number}")
 
-        def empty(banks, dst, copy=nc.scalar.copy):
-            for acc, cols in banks:
-                copy(dst[:, cols], acc[:, cols])
+        def product(acc, weights, cols=WHOLE, start=True, stop=True):
+            codes, plane = weights
+            nc.tensor.matmul_mx(
+                out=acc[:, cols],
+                lhsT=codes.bitcast(FP8X4),
+                lhsT_scale=plane,
+                rhs=x_codes[:, cols].bitcast(FP8X4),
+                rhs_scale=x_plane[:, cols],
+                start=start,
+                stop=stop,
+            )
+            return acc
+
+        def negate(dst, src):
+            nc.scalar.activation(dst, src, COPY, scale=-1.0)
 
         nc.vector.tensor_copy(picked[:], scale_win[:].indirect(offs_t[:]))
         for r in range(4):
@@ -106,52 +107,48 @@ def tile_picked_specacc_none_p_kernel(tc, x_words, x_scales, w1, w2, sh, offs, a
         nc.sync.dma_start(w2_early[:], w2_rows[:, :, 0 : N // 2])
         nc.sync.dma_start(w2_late[:], w2_rows[:, :, N // 2 : N])
         spread = keep.tile([P, 2, P], F32, name="spread", align_bytes=64)
-        mix = keep.tile([P, 2, V], F32, name="mix", align_bytes=64)
-        turned = psum.tile([P, S], F32, name="acc")
+        share = keep.tile([P, V], F32, name="share", align_bytes=64)
+        turned = bank(0)
         for c in range(2):
             nc.tensor.transpose(turned[:, c * P : (c + 1) * P], share_rows[:, c * P : (c + 1) * P], ident[:])
         nc.scalar.copy(
             spread[:].rearrange("p c (g r) -> p c g r", r=16),
             turned[:, 0:V].rearrange("p (c k o) -> p c k o", c=2, o=1)[:, :, 88:96, :].to_broadcast([P, 2, 8, 16]),
         )
-        back = psum.tile([P, S], F32, name="acc")
+        back = bank(1)
         for c in range(2):
             nc.tensor.transpose(back[:, c * P : (c + 1) * P], spread[:, c, :], ident[:])
-        nc.scalar.copy(mix[:, 1, :], back[:, 0:V])
-        nc.scalar.activation(mix[:, 0, :], back[:, 0:V], COPY, bias=1.0, scale=-1.0)
+        nc.scalar.copy(share[:], back[:, 0:V])
         round_tiles(nc.vector.tensor_copy, w1_raw, 0, slice(0, 2), w1_bf)
-        round_tiles(nc.scalar.copy, w1_raw, 0, slice(2, 4), w1_bf)
+        for t in range(2, TILES):
+            round_tiles(negate, w1_raw, 0, slice(t, t + 1), w1_bf)
         q1 = quantize(w1_bf[0], "w1_lo") + quantize(w1_bf[1], "w1_hi")
         for cols in HALVES:
             nc.vector.tensor_copy(
                 x_codes[:, cols], word_win[:].bitcast(U32).indirect(offs_t[:, cols.start // 16 : cols.stop // 16])
             )
 
-        y = [keep.tile([P, S], F32, name=f"y{t}", align_bytes=64) for t in range(2)]
-        e = [keep.tile([P, S], F32, name=f"e{t}", align_bytes=64) for t in range(TILES)]
-        found = [keep.tile([P, 2, V], F32, name=f"found{t}", align_bytes=64) for t in range(TILES)]
+        y = [keep.tile([P, S], F32, name=f"y{t}", align_bytes=64) for t in range(TILES)]
         out_t = out.rearrange("(a t i) s -> t a i s", t=TILES, i=2)
 
-        def fetch(t, side, rows):
-            nc.scalar.activation(found[t][:, side, :], rows[t][:].indirect(acc_t[:]), COPY)
+        def fetch(dst, rows):
+            nc.scalar.activation(dst[:], rows[:].indirect(acc_t[:]), COPY)
 
-        y_banks = [product(q1[t], HALVES if t == 0 else [WHOLE]) for t in range(TILES)]
-        for t in range(2):
-            empty(y_banks[t], y[t])
-        for t in range(2):
-            fetch(t, 0, y)
+        for half, cols in enumerate(HALVES):
+            nc.scalar.copy(y[0][:, cols], product(bank(half), q1[0], cols)[:, cols])
+        nc.scalar.copy(y[1][:], product(bank(2), q1[1])[:])
+        y_found = {0: keep.tile([P, V], F32, name="y_found0", align_bytes=64)}
+        fetch(y_found[0], y[0])
+        negate(y[2][:], product(bank(3), q1[2])[:])
 
-        w2_codes = [
-            reuse.tile([P, P], U32, name=f"w2_codes{t}", align_bytes=64, offset=at)
-            for t, at in enumerate((12288, 13824, 12800, 13312))
-        ]
+        w2_codes = keep.tile([P, TILES, P], U32, name="w2_codes", align_bytes=64)
         w2_plane = keep.tile([P, TILES, P], U8, name="w2_plane", align_bytes=64)
 
         def quantize_half(t, half):
             cols = slice(half * P // 2, (half + 1) * P // 2)
             first = ((t % PAIR) * P + cols.start) * PACK
             nc.vector.quantize_mx(
-                out=w2_codes[t][:, cols].bitcast(FP8X4),
+                out=w2_codes[:, t, cols].bitcast(FP8X4),
                 scales=w2_plane[:, t, cols],
                 in_=w2_bf[t // PAIR][:, first : first + P // 2 * PACK],
             )
@@ -161,27 +158,37 @@ def tile_picked_specacc_none_p_kernel(tc, x_words, x_scales, w1, w2, sh, offs, a
                 round_tiles(nc.vector.tensor_copy, raw, half * P // 2, slice(2 * pair, 2 * pair + 2), w2_bf)
             for t in range(TILES):
                 quantize_half(t, half)
-        q2 = [(w2_codes[t][:], w2_plane[:, t, :]) for t in range(TILES)]
-        e_banks = [product(q2[t], [WHOLE]) for t in range(TILES)]
-        y += [reuse.tile([P, S], F32, name=f"y{t}", align_bytes=64, offset=4096 + 2048 * t) for t in range(2, TILES)]
-        pulls = [keep.tile([P, V], F32, name=f"pull{t}", align_bytes=64) for t in range(2)]
-        terms = {t: keep.tile([P, 2, V], F32, name=f"terms{t}", align_bytes=64) for t in range(2, TILES)}
+        q2 = [(w2_codes[:, t, :], w2_plane[:, t, :]) for t in range(TILES)]
 
-        def put(t, first, second):
-            nc.vector.tensor_tensor(y[t][:].indirect(acc_t[:]), first, second, ADD)
+        gap = [reuse.tile([P, S], F32, name=f"gap{t}", align_bytes=64, offset=8192 + 2048 * t) for t in range(TILES)]
+        pull = [keep.tile([P, V], F32, name=f"pull{t}", align_bytes=64) for t in range(TILES)]
+        gap_found = {t: keep.tile([P, V], F32, name=f"gap_found{t}", align_bytes=64) for t in range(2, TILES)}
+
+        def gap_product(number, t):
+            acc = product(bank(number), q2[t], stop=False)
+            return product(acc, q1[t], start=False)
+
+        def put(t):
+            nc.vector.tensor_tensor(y[t][:].indirect(acc_t[:]), y_found[t][:], pull[t][:], ADD)
             nc.sync.dma_start(out_t[t], y[t][:])
 
         for t in range(2):
-            nc.vector.tensor_tensor(e[t][:], e_banks[t][0][0][:], y[t][:], SUB)
+            nc.vector.tensor_tensor(gap[t][:], product(bank(4 + t), q2[t])[:], y[t][:], SUB)
         for t in range(2):
-            nc.vector.tensor_tensor(pulls[t][:], e[t][:].indirect(acc_t[:]), mix[:, 1, :], MULT)
+            nc.vector.tensor_tensor(pull[t][:], gap[t][:].indirect(acc_t[:]), share[:], MULT)
+        y_found[1] = keep.tile([P, V], F32, name="y_found1", align_bytes=64)
+        fetch(y_found[1], y[1])
         for t in range(2, TILES):
-            empty(y_banks[t], y[t])
-            empty(e_banks[t], e[t])
-            fetch(t, 0, y)
-            fetch(t, 1, e)
+            nc.scalar.copy(gap[t][:], gap_product(4 + t, t)[:])
+        fetch(gap_found[2], gap[2])
+        negate(y[3][:], product(bank(4), q1[3])[:])
+        fetch(gap_found[3], gap[3])
+        for t in range(2, TILES):
+            y_found[t] = reuse.tile([P, V], F32, name=f"y_found{t}", align_bytes=64, offset=12288 + 1024 * t)
+            fetch(y_found[t], y[t])
         for t in range(2):
-            put(t, found[t][:, 0, :], pulls[t][:])
-            nc.vector.tensor_tensor(terms[t + 2][:], found[t + 2][:], mix[:], MULT)
+            put(t)
         for t in range(2, TILES):
-            put(t, terms[t][:, 0, :], terms[t][:, 1, :])
+            nc.vector.tensor_tensor(pull[t][:], gap_found[t][:], share[:], MULT)
+        for t in range(2, TILES):
+            put(t)

@@ -43,7 +43,10 @@ def tile_picked_specacc_none_p_kernel(tc, x_words, x_scales, w1, w2, sh, offs, a
         x_codes = keep.tile([P, S], U32, name="x_codes", align_bytes=64)
         x_plane = keep.tile([P, S], U8, name="x_plane", align_bytes=64)
         w1_bf = [keep.tile([P, PAIR * P * PACK], BF16, name=f"w1_bf{a}", align_bytes=64) for a in range(2)]
-        w2_bf = [keep.tile([P, PAIR * P * PACK], BF16, name=f"w2_bf{a}", align_bytes=64) for a in range(2)]
+        w2_bf = [
+            reuse.tile([P, PAIR * P * PACK], BF16, name=f"w2_bf{a}", align_bytes=64, offset=16384 + 2048 * a)
+            for a in range(2)
+        ]
         scale_win = reuse.tile([P, T], U8, name="scale_win", align_bytes=64, offset=3584)
 
         nc.scalar.dma_start(scale_win[16:32, :].bitcast(I32), x_scales[0].bitcast(I32))
@@ -108,6 +111,7 @@ def tile_picked_specacc_none_p_kernel(tc, x_words, x_scales, w1, w2, sh, offs, a
         nc.sync.dma_start(w2_late[:], w2_rows[:, :, N // 2 : N])
         spread = keep.tile([P, 2, P], F32, name="spread", align_bytes=64)
         share = keep.tile([P, V], F32, name="share", align_bytes=64)
+        rest = keep.tile([P, V], F32, name="rest", align_bytes=64)
         turned = bank(0)
         for c in range(2):
             nc.tensor.transpose(turned[:, c * P : (c + 1) * P], share_rows[:, c * P : (c + 1) * P], ident[:])
@@ -119,6 +123,7 @@ def tile_picked_specacc_none_p_kernel(tc, x_words, x_scales, w1, w2, sh, offs, a
         for c in range(2):
             nc.tensor.transpose(back[:, c * P : (c + 1) * P], spread[:, c, :], ident[:])
         nc.scalar.copy(share[:], back[:, 0:V])
+        nc.scalar.activation(rest[:], back[:, 0:V], COPY, bias=1.0, scale=-1.0)
         round_tiles(nc.vector.tensor_copy, w1_raw, 0, slice(0, 2), w1_bf)
         for t in range(2, TILES):
             round_tiles(negate, w1_raw, 0, slice(t, t + 1), w1_bf)
@@ -137,8 +142,6 @@ def tile_picked_specacc_none_p_kernel(tc, x_words, x_scales, w1, w2, sh, offs, a
         for half, cols in enumerate(HALVES):
             nc.scalar.copy(y[0][:, cols], product(bank(half), q1[0], cols)[:, cols])
         nc.scalar.copy(y[1][:], product(bank(2), q1[1])[:])
-        y_found = {0: keep.tile([P, V], F32, name="y_found0", align_bytes=64)}
-        fetch(y_found[0], y[0])
         negate(y[2][:], product(bank(3), q1[2])[:])
 
         w2_codes = keep.tile([P, TILES, P], U32, name="w2_codes", align_bytes=64)
@@ -153,11 +156,22 @@ def tile_picked_specacc_none_p_kernel(tc, x_words, x_scales, w1, w2, sh, offs, a
                 in_=w2_bf[t // PAIR][:, first : first + P // 2 * PACK],
             )
 
-        for half, raw in enumerate((w2_early, w2_late)):
-            for pair in range(2):
-                round_tiles(nc.vector.tensor_copy, raw, half * P // 2, slice(2 * pair, 2 * pair + 2), w2_bf)
-            for t in range(TILES):
-                quantize_half(t, half)
+        for pair in range(2):
+            round_tiles(nc.vector.tensor_copy, w2_early, 0, slice(2 * pair, 2 * pair + 2), w2_bf)
+        for t in range(TILES):
+            quantize_half(t, 0)
+        for t in range(2):
+            round_tiles(nc.vector.tensor_copy, w2_late, P // 2, slice(t, t + 1), w2_bf)
+        for t in range(2):
+            quantize_half(t, 1)
+        round_tiles(nc.vector.tensor_copy, w2_late, P // 2, slice(2, TILES), w2_bf)
+        y_found = {
+            t: reuse.tile([P, V], F32, name=f"y_found{t}", align_bytes=64, offset=16384 + 1024 * t) for t in range(2)
+        }
+        nc.vector.tensor_tensor(y_found[0][:], y[0][:].indirect(acc_t[:]), rest[:], MULT)
+        for t in range(2, TILES):
+            quantize_half(t, 1)
+        nc.vector.tensor_tensor(y_found[1][:], y[1][:].indirect(acc_t[:]), rest[:], MULT)
         q2 = [(w2_codes[:, t, :], w2_plane[:, t, :]) for t in range(TILES)]
 
         gap = [reuse.tile([P, S], F32, name=f"gap{t}", align_bytes=64, offset=8192 + 2048 * t) for t in range(TILES)]
@@ -172,12 +186,11 @@ def tile_picked_specacc_none_p_kernel(tc, x_words, x_scales, w1, w2, sh, offs, a
             nc.vector.tensor_tensor(y[t][:].indirect(acc_t[:]), y_found[t][:], pull[t][:], ADD)
             nc.sync.dma_start(out_t[t], y[t][:])
 
-        for t in range(2):
-            nc.vector.tensor_tensor(gap[t][:], product(bank(4 + t), q2[t])[:], y[t][:], SUB)
+        for half, cols in enumerate(HALVES):
+            for t in range(2):
+                nc.scalar.copy(gap[t][:, cols], product(bank(4 - 4 * half + t), q2[t], cols)[:, cols])
         for t in range(2):
             nc.vector.tensor_tensor(pull[t][:], gap[t][:].indirect(acc_t[:]), share[:], MULT)
-        y_found[1] = keep.tile([P, V], F32, name="y_found1", align_bytes=64)
-        fetch(y_found[1], y[1])
         for t in range(2, TILES):
             nc.scalar.copy(gap[t][:], gap_product(4 + t, t)[:])
         fetch(gap_found[2], gap[2])

@@ -144,8 +144,8 @@ def tile_picked_specacc_none_p_kernel(tc, x_words, x_scales, w1, w2, sh, offs, a
         nc.scalar.copy(y[1][:], product(bank(2), q1[1])[:])
         negate(y[2][:], product(bank(3), q1[2])[:])
 
-        w2_codes = keep.tile([P, TILES, P], U32, name="w2_codes", align_bytes=64)
-        w2_plane = keep.tile([P, TILES, P], U8, name="w2_plane", align_bytes=64)
+        w2_codes = keep.tile([P, PAIR, P], U32, name="w2_codes", align_bytes=64)
+        w2_plane = keep.tile([P, PAIR, P], U8, name="w2_plane", align_bytes=64)
 
         def quantize_half(t, half):
             cols = slice(half * P // 2, (half + 1) * P // 2)
@@ -158,7 +158,7 @@ def tile_picked_specacc_none_p_kernel(tc, x_words, x_scales, w1, w2, sh, offs, a
 
         for pair in range(2):
             round_tiles(nc.vector.tensor_copy, w2_early, 0, slice(2 * pair, 2 * pair + 2), w2_bf)
-        for t in range(TILES):
+        for t in range(2):
             quantize_half(t, 0)
         for t in range(2):
             round_tiles(nc.vector.tensor_copy, w2_late, P // 2, slice(t, t + 1), w2_bf)
@@ -169,14 +169,12 @@ def tile_picked_specacc_none_p_kernel(tc, x_words, x_scales, w1, w2, sh, offs, a
             t: reuse.tile([P, V], F32, name=f"y_found{t}", align_bytes=64, offset=16384 + 1024 * t) for t in range(2)
         }
         nc.vector.tensor_tensor(y_found[0][:], y[0][:].indirect(acc_t[:]), rest[:], MULT)
-        for t in range(2, TILES):
-            quantize_half(t, 1)
+        q2 = [(w2_codes[:, t, :], w2_plane[:, t, :]) for t in range(2)] + quantize(w2_bf[1], "w2_hi")
         nc.vector.tensor_tensor(y_found[1][:], y[1][:].indirect(acc_t[:]), rest[:], MULT)
-        q2 = [(w2_codes[:, t, :], w2_plane[:, t, :]) for t in range(TILES)]
 
         gap = [reuse.tile([P, S], F32, name=f"gap{t}", align_bytes=64, offset=8192 + 2048 * t) for t in range(TILES)]
         pull = [keep.tile([P, V], F32, name=f"pull{t}", align_bytes=64) for t in range(TILES)]
-        gap_found = {t: keep.tile([P, V], F32, name=f"gap_found{t}", align_bytes=64) for t in range(2, TILES)}
+        gap_found = {t: keep.tile([P, V], F32, name=f"gap_found{t}", align_bytes=64) for t in range(1, TILES)}
 
         def gap_product(number, t):
             acc = product(bank(number), q2[t], stop=False)
@@ -186,22 +184,26 @@ def tile_picked_specacc_none_p_kernel(tc, x_words, x_scales, w1, w2, sh, offs, a
             nc.vector.tensor_tensor(y[t][:].indirect(acc_t[:]), y_found[t][:], pull[t][:], ADD)
             nc.sync.dma_start(out_t[t], y[t][:])
 
+        def weigh(t):
+            nc.vector.tensor_tensor(pull[t][:], gap_found[t][:], share[:], MULT)
+
         for half, cols in enumerate(HALVES):
-            for t in range(2):
-                nc.scalar.copy(gap[t][:, cols], product(bank(4 - 4 * half + t), q2[t], cols)[:, cols])
-        for t in range(2):
-            nc.vector.tensor_tensor(pull[t][:], gap[t][:].indirect(acc_t[:]), share[:], MULT)
-        for t in range(2, TILES):
-            nc.scalar.copy(gap[t][:], gap_product(4 + t, t)[:])
-        fetch(gap_found[2], gap[2])
+            nc.scalar.copy(gap[0][:, cols], product(bank(4 + half), q2[0], cols)[:, cols])
+        nc.vector.tensor_tensor(pull[0][:], gap[0][:].indirect(acc_t[:]), share[:], MULT)
+        nc.scalar.copy(gap[1][:], product(bank(0), q2[1])[:])
+        nc.scalar.copy(gap[2][:], gap_product(6, 2)[:])
+        for t in range(1, 3):
+            fetch(gap_found[t], gap[t])
+        nc.scalar.copy(gap[3][:], gap_product(7, 3)[:])
         negate(y[3][:], product(bank(4), q1[3])[:])
         fetch(gap_found[3], gap[3])
         for t in range(2, TILES):
             y_found[t] = reuse.tile([P, V], F32, name=f"y_found{t}", align_bytes=64, offset=12288 + 1024 * t)
             fetch(y_found[t], y[t])
-        for t in range(2):
-            put(t)
-        for t in range(2, TILES):
-            nc.vector.tensor_tensor(pull[t][:], gap_found[t][:], share[:], MULT)
-        for t in range(2, TILES):
-            put(t)
+        put(0)
+        weigh(1)
+        weigh(2)
+        put(1)
+        weigh(3)
+        put(2)
+        put(3)

@@ -181,29 +181,31 @@ def tile_picked_specacc_none_p_kernel(tc, x_words, x_scales, w1, w2, sh, offs, a
             return product(acc, q1[t], start=False)
 
         def put(t):
-            nc.vector.tensor_tensor(y[t][:].indirect(acc_t[:]), y_found[t][:], pull[t][:], ADD)
+            nc.vector.tensor_copy(y[t][:].indirect(acc_t[:]), mixed[t][:])
             nc.sync.dma_start(out_t[t], y[t][:])
 
-        def weigh(t):
-            nc.vector.tensor_tensor(pull[t][:], gap_found[t][:], share[:], MULT)
+        mixed = [keep.tile([P, V], F32, name=f"mixed{t}", align_bytes=64) for t in range(TILES)]
+
+        def mix(t):
+            nc.gpsimd.tensor_tensor(pull[t][:], gap_found[t][:], share[:], MULT)
+            nc.gpsimd.tensor_tensor(mixed[t][:], y_found[t][:], pull[t][:], ADD)
 
         for half, cols in enumerate(HALVES):
             nc.scalar.copy(gap[0][:, cols], product(bank(4 + half), q2[0], cols)[:, cols])
         nc.vector.tensor_tensor(pull[0][:], gap[0][:].indirect(acc_t[:]), share[:], MULT)
+        nc.vector.tensor_tensor(mixed[0][:], y_found[0][:], pull[0][:], ADD)
+        for t in range(2, TILES):
+            y_found[t] = reuse.tile([P, V], F32, name=f"y_found{t}", align_bytes=64, offset=8192 + 1024 * (t - 2))
         nc.scalar.copy(gap[1][:], product(bank(0), q2[1])[:])
         nc.scalar.copy(gap[2][:], gap_product(6, 2)[:])
-        for t in range(1, 3):
-            fetch(gap_found[t], gap[t])
+        fetch(gap_found[1], gap[1])
+        fetch(y_found[2], y[2])
+        fetch(gap_found[2], gap[2])
         nc.scalar.copy(gap[3][:], gap_product(7, 3)[:])
         negate(y[3][:], product(bank(4), q1[3])[:])
         fetch(gap_found[3], gap[3])
-        for t in range(2, TILES):
-            y_found[t] = reuse.tile([P, V], F32, name=f"y_found{t}", align_bytes=64, offset=12288 + 1024 * t)
-            fetch(y_found[t], y[t])
-        put(0)
-        weigh(1)
-        weigh(2)
-        put(1)
-        weigh(3)
-        put(2)
-        put(3)
+        fetch(y_found[3], y[3])
+        for t in range(1, TILES):
+            mix(t)
+        for t in range(TILES):
+            put(t)

@@ -172,8 +172,14 @@ def tile_picked_specacc_none_p_kernel(tc, x_words, x_scales, w1, w2, sh, offs, a
         q2 = [(w2_codes[:, t, :], w2_plane[:, t, :]) for t in range(2)] + quantize(w2_bf[1], "w2_hi")
         nc.vector.tensor_tensor(y_found[1][:], y[1][:].indirect(acc_t[:]), rest[:], MULT)
 
-        gap = [reuse.tile([P, S], F32, name=f"gap{t}", align_bytes=64, offset=8192 + 2048 * t) for t in range(TILES)]
-        pull = [keep.tile([P, V], F32, name=f"pull{t}", align_bytes=64) for t in range(TILES)]
+        gap = [
+            reuse.tile([P, S], F32, name=f"gap{t}", align_bytes=64, offset=at)
+            for t, at in enumerate((8192, 12224, 10240, 14208))
+        ]
+        pull = [
+            reuse.tile([P, V], F32, name=f"pull{t}", align_bytes=64, offset=at)
+            for t, at in enumerate((20480, 22016, 21504, 22528))
+        ]
         gap_found = {t: keep.tile([P, V], F32, name=f"gap_found{t}", align_bytes=64) for t in range(1, TILES)}
 
         def gap_product(number, t):
@@ -181,31 +187,38 @@ def tile_picked_specacc_none_p_kernel(tc, x_words, x_scales, w1, w2, sh, offs, a
             return product(acc, q1[t], start=False)
 
         def put(t):
-            nc.vector.tensor_copy(y[t][:].indirect(acc_t[:]), mixed[t][:])
+            nc.vector.tensor_tensor(y[t][:].indirect(acc_t[:]), y_found[t][:], pull[t][:], ADD)
             nc.sync.dma_start(out_t[t], y[t][:])
 
-        mixed = [keep.tile([P, V], F32, name=f"mixed{t}", align_bytes=64) for t in range(TILES)]
+        mixed = [keep.tile([P, V], F32, name=f"mixed{t}", align_bytes=64) for t in range(PAIR)]
 
-        def mix(t):
+        def weigh(t):
             nc.gpsimd.tensor_tensor(pull[t][:], gap_found[t][:], share[:], MULT)
-            nc.gpsimd.tensor_tensor(mixed[t][:], y_found[t][:], pull[t][:], ADD)
+
+        def place(t):
+            nc.vector.tensor_copy(y[t][:].indirect(acc_t[:]), mixed[t][:])
+            nc.sync.dma_start(out_t[t], y[t][:])
 
         for half, cols in enumerate(HALVES):
             nc.scalar.copy(gap[0][:, cols], product(bank(4 + half), q2[0], cols)[:, cols])
         nc.vector.tensor_tensor(pull[0][:], gap[0][:].indirect(acc_t[:]), share[:], MULT)
         nc.vector.tensor_tensor(mixed[0][:], y_found[0][:], pull[0][:], ADD)
-        for t in range(2, TILES):
-            y_found[t] = reuse.tile([P, V], F32, name=f"y_found{t}", align_bytes=64, offset=8192 + 1024 * (t - 2))
         nc.scalar.copy(gap[1][:], product(bank(0), q2[1])[:])
-        nc.scalar.copy(gap[2][:], gap_product(6, 2)[:])
         fetch(gap_found[1], gap[1])
+        for t in range(PAIR, TILES):
+            nc.scalar.copy(gap[t][:], gap_product(4 + t, t)[:])
+        for t in range(PAIR, TILES):
+            fetch(gap_found[t], gap[t])
+        y_found[2] = reuse.tile([P, V], F32, name="y_found2", align_bytes=64, offset=12800)
         fetch(y_found[2], y[2])
-        fetch(gap_found[2], gap[2])
-        nc.scalar.copy(gap[3][:], gap_product(7, 3)[:])
-        negate(y[3][:], product(bank(4), q1[3])[:])
-        fetch(gap_found[3], gap[3])
+        negate(y[3][:], product(bank(6), q1[3])[:])
+        y_found[3] = keep.tile([P, V], F32, name="y_found3", align_bytes=64)
         fetch(y_found[3], y[3])
-        for t in range(1, TILES):
-            mix(t)
-        for t in range(TILES):
+        weigh(1)
+        nc.gpsimd.tensor_tensor(mixed[1][:], y_found[1][:], pull[1][:], ADD)
+        for t in range(PAIR, TILES):
+            weigh(t)
+        for t in range(PAIR):
+            place(t)
+        for t in range(PAIR, TILES):
             put(t)

@@ -76,8 +76,9 @@ def tile_picked_specacc_none_p_kernel(tc, x_words, x_scales, w1, w2, sh, offs, a
             else:
                 copy(dst[:, :, first // 2 : first // 2 + count], src[:, tiles])
 
-        def quantize(grouped, name):
-            codes = keep.tile([P, PAIR * P], U32, name=name + "_codes", align_bytes=64)
+        def quantize(grouped, name, **place):
+            pool = reuse if place else keep
+            codes = pool.tile([P, PAIR * P], U32, name=name + "_codes", align_bytes=64, **place)
             plane = keep.tile([P, PAIR * P], U8, name=name + "_plane", align_bytes=64)
             nc.vector.quantize_mx(out=codes[:].bitcast(FP8X4), scales=plane[:], in_=grouped[:])
             return [(codes[:, i * P : (i + 1) * P], plane[:, i * P : (i + 1) * P]) for i in range(PAIR)]
@@ -169,18 +170,14 @@ def tile_picked_specacc_none_p_kernel(tc, x_words, x_scales, w1, w2, sh, offs, a
             t: reuse.tile([P, V], F32, name=f"y_found{t}", align_bytes=64, offset=16384 + 1024 * t) for t in range(2)
         }
         nc.vector.tensor_tensor(y_found[0][:], y[0][:].indirect(acc_t[:]), rest[:], MULT)
-        q2 = [(w2_codes[:, t, :], w2_plane[:, t, :]) for t in range(2)] + quantize(w2_bf[1], "w2_hi")
+        q2 = [(w2_codes[:, t, :], w2_plane[:, t, :]) for t in range(2)] + quantize(w2_bf[1], "w2_hi", offset=20480)
         nc.vector.tensor_tensor(y_found[1][:], y[1][:].indirect(acc_t[:]), rest[:], MULT)
 
-        gap = [
-            reuse.tile([P, S], F32, name=f"gap{t}", align_bytes=64, offset=at)
-            for t, at in enumerate((8192, 12224, 10240, 14208))
-        ]
-        pull = [
-            reuse.tile([P, V], F32, name=f"pull{t}", align_bytes=64, offset=at)
-            for t, at in enumerate((20480, 22016, 21504, 22528))
-        ]
-        gap_found = {t: keep.tile([P, V], F32, name=f"gap_found{t}", align_bytes=64) for t in range(1, TILES)}
+        gap = [reuse.tile([P, S], F32, name=f"gap{t}", align_bytes=64, offset=8192 + 2048 * t) for t in range(TILES)]
+        pull = [keep.tile([P, V], F32, name=f"pull{t}", align_bytes=64) for t in range(PAIR)]
+        gap_found = keep.tile([P, PAIR, V], F32, name="gap_found", align_bytes=64)
+        late_pull = keep.tile([P, PAIR, V], F32, name="late_pull", align_bytes=64)
+        pull += [late_pull[:, i, :] for i in range(PAIR)]
 
         def gap_product(number, t):
             acc = product(bank(number), q2[t], stop=False)
@@ -190,35 +187,27 @@ def tile_picked_specacc_none_p_kernel(tc, x_words, x_scales, w1, w2, sh, offs, a
             nc.vector.tensor_tensor(y[t][:].indirect(acc_t[:]), y_found[t][:], pull[t][:], ADD)
             nc.sync.dma_start(out_t[t], y[t][:])
 
-        mixed = [keep.tile([P, V], F32, name=f"mixed{t}", align_bytes=64) for t in range(PAIR)]
-
-        def weigh(t):
-            nc.gpsimd.tensor_tensor(pull[t][:], gap_found[t][:], share[:], MULT)
-
-        def place(t):
-            nc.vector.tensor_copy(y[t][:].indirect(acc_t[:]), mixed[t][:])
-            nc.sync.dma_start(out_t[t], y[t][:])
-
         for half, cols in enumerate(HALVES):
             nc.scalar.copy(gap[0][:, cols], product(bank(4 + half), q2[0], cols)[:, cols])
-        nc.vector.tensor_tensor(pull[0][:], gap[0][:].indirect(acc_t[:]), share[:], MULT)
-        nc.vector.tensor_tensor(mixed[0][:], y_found[0][:], pull[0][:], ADD)
         nc.scalar.copy(gap[1][:], product(bank(0), q2[1])[:])
-        fetch(gap_found[1], gap[1])
-        for t in range(PAIR, TILES):
-            nc.scalar.copy(gap[t][:], gap_product(4 + t, t)[:])
-        for t in range(PAIR, TILES):
-            fetch(gap_found[t], gap[t])
-        y_found[2] = reuse.tile([P, V], F32, name="y_found2", align_bytes=64, offset=12800)
-        fetch(y_found[2], y[2])
-        negate(y[3][:], product(bank(6), q1[3])[:])
-        y_found[3] = keep.tile([P, V], F32, name="y_found3", align_bytes=64)
-        fetch(y_found[3], y[3])
-        weigh(1)
-        nc.gpsimd.tensor_tensor(mixed[1][:], y_found[1][:], pull[1][:], ADD)
-        for t in range(PAIR, TILES):
-            weigh(t)
         for t in range(PAIR):
-            place(t)
+            nc.vector.tensor_tensor(pull[t][:], gap[t][:].indirect(acc_t[:]), share[:], MULT)
+        nc.scalar.copy(gap[2][:], gap_product(6, 2)[:])
+        y3_bank = product(bank(4), q1[3])
+        nc.scalar.copy(gap[3][:], gap_product(7, 3)[:])
+        mixed = reuse.tile([P, V], F32, name="mixed", align_bytes=64, offset=20480)
+        nc.vector.tensor_tensor(mixed[:], y_found[0][:], pull[0][:], ADD)
+        for t in range(PAIR, TILES):
+            fetch(gap_found[:, t - PAIR, :], gap[t])
+        nc.gpsimd.tensor_tensor(
+            late_pull[:], gap_found[:], share[:].rearrange("p (o v) -> p o v", o=1).to_broadcast([P, PAIR, V]), MULT
+        )
+        negate(y[3][:], y3_bank[:])
+        for t in range(PAIR, TILES):
+            y_found[t] = reuse.tile([P, V], F32, name=f"y_found{t}", align_bytes=64, offset=6144 + 1024 * t)
+            fetch(y_found[t], y[t])
+        put(1)
+        nc.vector.tensor_copy(y[0][:].indirect(acc_t[:]), mixed[:])
+        nc.sync.dma_start(out_t[0], y[0][:])
         for t in range(PAIR, TILES):
             put(t)

@@ -134,7 +134,7 @@ def tile_picked_specacc_none_p_kernel(tc, x_words, x_scales, w1, w2, sh, offs, a
                 x_codes[:, cols], word_win[:].bitcast(U32).indirect(offs_t[:, cols.start // 16 : cols.stop // 16])
             )
 
-        y = [keep.tile([P, S], F32, name=f"y{t}", align_bytes=64) for t in range(TILES)]
+        y = [keep.tile([P, S], F32, name=f"y{t}", align_bytes=64) for t in range(TILES - 1)]
         out_t = out.rearrange("(a t i) s -> t a i s", t=TILES, i=2)
 
         def fetch(dst, rows):
@@ -187,14 +187,15 @@ def tile_picked_specacc_none_p_kernel(tc, x_words, x_scales, w1, w2, sh, offs, a
             nc.vector.tensor_tensor(y[t][:].indirect(acc_t[:]), y_found[t][:], pull[t][:], ADD)
             nc.sync.dma_start(out_t[t], y[t][:])
 
-        for half, cols in enumerate(HALVES):
-            nc.scalar.copy(gap[0][:, cols], product(bank(4 + half), q2[0], cols)[:, cols])
-        nc.scalar.copy(gap[1][:], product(bank(0), q2[1])[:])
+        for t in range(PAIR):
+            for half, cols in enumerate(HALVES):
+                nc.scalar.copy(gap[t][:, cols], product(bank(4 - 4 * t + half), q2[t], cols)[:, cols])
         for t in range(PAIR):
             nc.vector.tensor_tensor(pull[t][:], gap[t][:].indirect(acc_t[:]), share[:], MULT)
         nc.scalar.copy(gap[2][:], gap_product(6, 2)[:])
-        y3_bank = product(bank(4), q1[3])
+        y3_bank = product(bank(4), q1[3], HALVES[0])
         nc.scalar.copy(gap[3][:], gap_product(7, 3)[:])
+        product(y3_bank, q1[3], HALVES[1])
         mixed = reuse.tile([P, V], F32, name="mixed", align_bytes=64, offset=20480)
         nc.vector.tensor_tensor(mixed[:], y_found[0][:], pull[0][:], ADD)
         for t in range(PAIR, TILES):
@@ -202,9 +203,10 @@ def tile_picked_specacc_none_p_kernel(tc, x_words, x_scales, w1, w2, sh, offs, a
         nc.gpsimd.tensor_tensor(
             late_pull[:], gap_found[:], share[:].rearrange("p (o v) -> p o v", o=1).to_broadcast([P, PAIR, V]), MULT
         )
+        y.append(reuse.tile([P, S], F32, name="y3", align_bytes=64, offset=12288))
         negate(y[3][:], y3_bank[:])
         for t in range(PAIR, TILES):
-            y_found[t] = reuse.tile([P, V], F32, name=f"y_found{t}", align_bytes=64, offset=6144 + 1024 * t)
+            y_found[t] = reuse.tile([P, V], F32, name=f"y_found{t}", align_bytes=64, offset=12288 + 1024 * t)
             fetch(y_found[t], y[t])
         put(1)
         nc.vector.tensor_copy(y[0][:].indirect(acc_t[:]), mixed[:])

@@ -134,7 +134,7 @@ def tile_picked_specacc_none_p_kernel(tc, x_words, x_scales, w1, w2, sh, offs, a
                 x_codes[:, cols], word_win[:].bitcast(U32).indirect(offs_t[:, cols.start // 16 : cols.stop // 16])
             )
 
-        y = [keep.tile([P, S], F32, name=f"y{t}", align_bytes=64) for t in range(TILES - 1)]
+        y = [keep.tile([P, S], F32, name=f"y{t}", align_bytes=64) for t in range(PAIR)]
         out_t = out.rearrange("(a t i) s -> t a i s", t=TILES, i=2)
 
         def fetch(dst, rows):
@@ -143,7 +143,7 @@ def tile_picked_specacc_none_p_kernel(tc, x_words, x_scales, w1, w2, sh, offs, a
         for half, cols in enumerate(HALVES):
             nc.scalar.copy(y[0][:, cols], product(bank(half), q1[0], cols)[:, cols])
         nc.scalar.copy(y[1][:], product(bank(2), q1[1])[:])
-        negate(y[2][:], product(bank(3), q1[2])[:])
+        y2_bank = product(bank(3), q1[2])
 
         w2_codes = keep.tile([P, PAIR, P], U32, name="w2_codes", align_bytes=64)
         w2_plane = keep.tile([P, PAIR, P], U8, name="w2_plane", align_bytes=64)
@@ -203,10 +203,11 @@ def tile_picked_specacc_none_p_kernel(tc, x_words, x_scales, w1, w2, sh, offs, a
         nc.gpsimd.tensor_tensor(
             late_pull[:], gap_found[:], share[:].rearrange("p (o v) -> p o v", o=1).to_broadcast([P, PAIR, V]), MULT
         )
-        y.append(reuse.tile([P, S], F32, name="y3", align_bytes=64, offset=12288))
-        negate(y[3][:], y3_bank[:])
+        for t, acc, at in ((2, y2_bank, 11264), (3, y3_bank, 13312)):
+            y.append(reuse.tile([P, S], F32, name=f"y{t}", align_bytes=64, offset=at))
+            negate(y[t][:], acc[:])
         for t in range(PAIR, TILES):
-            y_found[t] = reuse.tile([P, V], F32, name=f"y_found{t}", align_bytes=64, offset=12288 + 1024 * t)
+            y_found[t] = keep.tile([P, V], F32, name=f"y_found{t}", align_bytes=64)
             fetch(y_found[t], y[t])
         put(1)
         nc.vector.tensor_copy(y[0][:].indirect(acc_t[:]), mixed[:])

@@ -141,9 +141,9 @@ def tile_picked_specacc_none_p_kernel(tc, x_words, x_scales, w1, w2, sh, offs, a
             nc.scalar.activation(dst[:], rows[:].indirect(acc_t[:]), COPY)
 
         for half, cols in enumerate(HALVES):
-            nc.scalar.copy(y[0][:, cols], product(bank(half), q1[0], cols)[:, cols])
-        nc.scalar.copy(y[1][:], product(bank(2), q1[1])[:])
-        y2_bank = product(bank(3), q1[2])
+            nc.scalar.copy(y[0][:, cols], product(bank(2 + half), q1[0], cols)[:, cols])
+        nc.scalar.copy(y[1][:], product(bank(4), q1[1])[:])
+        y2_bank = product(bank(5), q1[2])
 
         w2_codes = keep.tile([P, PAIR, P], U32, name="w2_codes", align_bytes=64)
         w2_plane = keep.tile([P, PAIR, P], U8, name="w2_plane", align_bytes=64)
@@ -175,7 +175,7 @@ def tile_picked_specacc_none_p_kernel(tc, x_words, x_scales, w1, w2, sh, offs, a
 
         gap = [reuse.tile([P, S], F32, name=f"gap{t}", align_bytes=64, offset=8192 + 2048 * t) for t in range(TILES)]
         pull = [keep.tile([P, V], F32, name=f"pull{t}", align_bytes=64) for t in range(PAIR)]
-        gap_found = keep.tile([P, PAIR, V], F32, name="gap_found", align_bytes=64)
+        gap_found = reuse.tile([P, PAIR, V], F32, name="gap_found", align_bytes=64, offset=22528)
         late_pull = keep.tile([P, PAIR, V], F32, name="late_pull", align_bytes=64)
         pull += [late_pull[:, i, :] for i in range(PAIR)]
 
@@ -189,12 +189,12 @@ def tile_picked_specacc_none_p_kernel(tc, x_words, x_scales, w1, w2, sh, offs, a
 
         for t in range(PAIR):
             for half, cols in enumerate(HALVES):
-                nc.scalar.copy(gap[t][:, cols], product(bank(4 - 4 * t + half), q2[t], cols)[:, cols])
+                nc.scalar.copy(gap[t][:, cols], product(bank(6 - 6 * t + half), q2[t], cols)[:, cols])
         for t in range(PAIR):
             nc.vector.tensor_tensor(pull[t][:], gap[t][:].indirect(acc_t[:]), share[:], MULT)
-        nc.scalar.copy(gap[2][:], gap_product(6, 2)[:])
-        y3_bank = product(bank(4), q1[3], HALVES[0])
-        nc.scalar.copy(gap[3][:], gap_product(7, 3)[:])
+        nc.scalar.copy(gap[2][:], gap_product(2, 2)[:])
+        y3_bank = product(bank(6), q1[3], HALVES[0])
+        nc.scalar.copy(gap[3][:], gap_product(3, 3)[:])
         product(y3_bank, q1[3], HALVES[1])
         mixed = reuse.tile([P, V], F32, name="mixed", align_bytes=64, offset=20480)
         nc.vector.tensor_tensor(mixed[:], y_found[0][:], pull[0][:], ADD)
@@ -203,7 +203,7 @@ def tile_picked_specacc_none_p_kernel(tc, x_words, x_scales, w1, w2, sh, offs, a
         nc.gpsimd.tensor_tensor(
             late_pull[:], gap_found[:], share[:].rearrange("p (o v) -> p o v", o=1).to_broadcast([P, PAIR, V]), MULT
         )
-        for t, acc, at in ((2, y2_bank, 11264), (3, y3_bank, 13312)):
+        for t, acc, at in ((2, y2_bank, 12288), (3, y3_bank, 22528)):
             y.append(reuse.tile([P, S], F32, name=f"y{t}", align_bytes=64, offset=at))
             negate(y[t][:], acc[:])
         for t in range(PAIR, TILES):

@@ -134,7 +134,10 @@ def tile_picked_specacc_none_p_kernel(tc, x_words, x_scales, w1, w2, sh, offs, a
                 x_codes[:, cols], word_win[:].bitcast(U32).indirect(offs_t[:, cols.start // 16 : cols.stop // 16])
             )
 
-        y = [keep.tile([P, S], F32, name=f"y{t}", align_bytes=64) for t in range(PAIR)]
+        round_tiles(nc.scalar.copy, w2_early, 0, slice(PAIR, TILES), w2_bf)
+        for t in range(PAIR):
+            round_tiles(nc.vector.tensor_copy, w2_early, 0, slice(t, t + 1), w2_bf)
+        y = [reuse.tile([P, S], F32, name=f"y{t}", align_bytes=64, offset=2048 * t) for t in range(PAIR)]
         out_t = out.rearrange("(a t i) s -> t a i s", t=TILES, i=2)
 
         def fetch(dst, rows):
@@ -157,8 +160,6 @@ def tile_picked_specacc_none_p_kernel(tc, x_words, x_scales, w1, w2, sh, offs, a
                 in_=w2_bf[t // PAIR][:, first : first + P // 2 * PACK],
             )
 
-        for pair in range(2):
-            round_tiles(nc.vector.tensor_copy, w2_early, 0, slice(2 * pair, 2 * pair + 2), w2_bf)
         for t in range(2):
             quantize_half(t, 0)
         for t in range(2):
@@ -175,7 +176,7 @@ def tile_picked_specacc_none_p_kernel(tc, x_words, x_scales, w1, w2, sh, offs, a
 
         gap = [reuse.tile([P, S], F32, name=f"gap{t}", align_bytes=64, offset=8192 + 2048 * t) for t in range(TILES)]
         pull = [keep.tile([P, V], F32, name=f"pull{t}", align_bytes=64) for t in range(PAIR)]
-        gap_found = reuse.tile([P, PAIR, V], F32, name="gap_found", align_bytes=64, offset=22528)
+        gap_found = keep.tile([P, PAIR, V], F32, name="gap_found", align_bytes=64)
         late_pull = keep.tile([P, PAIR, V], F32, name="late_pull", align_bytes=64)
         pull += [late_pull[:, i, :] for i in range(PAIR)]
 
@@ -198,17 +199,18 @@ def tile_picked_specacc_none_p_kernel(tc, x_words, x_scales, w1, w2, sh, offs, a
         product(y3_bank, q1[3], HALVES[1])
         mixed = reuse.tile([P, V], F32, name="mixed", align_bytes=64, offset=20480)
         nc.vector.tensor_tensor(mixed[:], y_found[0][:], pull[0][:], ADD)
+        y.append(reuse.tile([P, S], F32, name="y2", align_bytes=64, offset=8192))
+        negate(y[2][:], y2_bank[:])
         for t in range(PAIR, TILES):
             fetch(gap_found[:, t - PAIR, :], gap[t])
-        nc.gpsimd.tensor_tensor(
-            late_pull[:], gap_found[:], share[:].rearrange("p (o v) -> p o v", o=1).to_broadcast([P, PAIR, V]), MULT
-        )
-        for t, acc, at in ((2, y2_bank, 12288), (3, y3_bank, 22528)):
-            y.append(reuse.tile([P, S], F32, name=f"y{t}", align_bytes=64, offset=at))
-            negate(y[t][:], acc[:])
-        for t in range(PAIR, TILES):
-            y_found[t] = keep.tile([P, V], F32, name=f"y_found{t}", align_bytes=64)
-            fetch(y_found[t], y[t])
+        for i in range(PAIR):
+            nc.gpsimd.tensor_tensor(late_pull[:, i, :], gap_found[:, i, :], share[:], MULT)
+        y_found[2] = reuse.tile([P, V], F32, name="y_found2", align_bytes=64, offset=14336)
+        fetch(y_found[2], y[2])
+        y.append(reuse.tile([P, S], F32, name="y3", align_bytes=64, offset=15360))
+        negate(y[3][:], y3_bank[:])
+        y_found[3] = keep.tile([P, V], F32, name="y_found3", align_bytes=64)
+        fetch(y_found[3], y[3])
         put(1)
         nc.vector.tensor_copy(y[0][:].indirect(acc_t[:]), mixed[:])
         nc.sync.dma_start(out_t[0], y[0][:])

from contextlib import ExitStack

import concourse.mybir as mybir
from concourse.masks import make_identity

K, T, S, V, N = 512, 2048, 512, 256, 512
FLOPS = 2 * 2 * K * N * S
BYTES = 128 * T * 4 + 16 * T + 2 * K * N * 4 + 8 * V * 4 + N * S * 4

F32 = mybir.dt.float32
BF16 = mybir.dt.bfloat16
I32 = mybir.dt.int32
U32 = mybir.dt.uint32
U16 = mybir.dt.uint16
U8 = mybir.dt.uint8
FP8X4 = mybir.dt.float8_e4m3fn_x4
MULT = mybir.AluOpType.mult
ADD = mybir.AluOpType.add
SUB = mybir.AluOpType.subtract
COPY = mybir.ActivationFunctionType.Copy

P = 128
PACK = 4
TILES = N // P
PAIR = 2
HALF = S // 2
WHOLE = slice(0, S)
HALVES = (slice(0, HALF), slice(HALF, S))


def tile_picked_specacc_none_p_kernel(tc, x_words, x_scales, w1, w2, sh, offs, acc_l, out):
    nc = tc.nc
    with ExitStack() as ctx:
        keep = ctx.enter_context(tc.tile_pool(name="keep", bufs=1))
        reuse = ctx.enter_context(tc.tile_pool(name="reuse", bufs=1))
        psum = ctx.enter_context(tc.psum_pool(name="psum", bufs=1))

        offs_t = keep.tile([P, S // 16], U16, name="offs_t")
        acc_t = keep.tile([P, V // 16], U16, name="acc_t")
        word_win = keep.tile([P, T], I32, name="word_win", align_bytes=64)
        w1_raw = keep.tile([P, PACK, N], F32, name="w1_raw", align_bytes=64)
        picked = keep.tile([P, S], U8, name="picked", align_bytes=64)
        x_codes = keep.tile([P, S], U32, name="x_codes", align_bytes=64)
        x_plane = keep.tile([P, S], U8, name="x_plane", align_bytes=64)
        w1_bf = [keep.tile([P, PAIR * P * PACK], BF16, name=f"w1_bf{a}", align_bytes=64) for a in range(2)]
        w2_bf = [
            reuse.tile([P, PAIR * P * PACK], BF16, name=f"w2_bf{a}", align_bytes=64, offset=16384 + 2048 * a)
            for a in range(2)
        ]
        scale_win = reuse.tile([P, T], U8, name="scale_win", align_bytes=64, offset=3584)

        nc.scalar.dma_start(scale_win[16:32, :].bitcast(I32), x_scales[0].bitcast(I32))
        nc.vector.memset(scale_win[0:16, :].bitcast(I32), 0)
        nc.vector.memset(scale_win[32:64, :].bitcast(I32), 0)
        nc.vector.memset(scale_win[64:P, :].bitcast(I32), 0)
        nc.vector.memset(x_plane[:].bitcast(I32), 0)
        share_rows = keep.tile([P, V], F32, name="share_rows", align_bytes=64)
        ident = keep.tile([P, P], F32, name="ident", align_bytes=64)
        nc.gpsimd.memset(share_rows[0:64, :], 0.0)
        nc.gpsimd.memset(share_rows[64:88, :], 0.0)
        nc.gpsimd.memset(share_rows[96:P, :], 0.0)
        make_identity(nc, ident[:])
        nc.sync.dma_start(offs_t[:], offs)
        nc.scalar.dma_start(share_rows[88:96, :], sh.rearrange("(g r) v -> g r v", r=64)[:, 0, :])
        nc.sync.dma_start(w1_raw[:], w1.rearrange("(p j) n -> p j n", j=PACK))
        nc.sync.dma_start(acc_t[:], acc_l)
        nc.sync.dma_start(word_win[:], x_words[0].rearrange("p n t -> p (n t)").bitcast(I32))

        def round_tiles(copy, raw, first, tiles, grouped):
            count = raw.shape[2] // (2 * TILES)
            pair, lo = divmod(tiles.start, PAIR)
            dst = grouped[pair][:].rearrange("p (t a i j) -> p t a j i", t=PAIR, i=2, j=PACK)
            src = raw[:].rearrange("p j (a t i) -> p t a j i", t=TILES, i=2)
            if tiles.stop - tiles.start == 1:
                copy(dst[:, lo, first // 2 : first // 2 + count], src[:, tiles.start])
            else:
                copy(dst[:, :, first // 2 : first // 2 + count], src[:, tiles])

        def quantize(grouped, name, **place):
            pool = reuse if place else keep
            codes = pool.tile([P, PAIR * P], U32, name=name + "_codes", align_bytes=64, **place)
            plane = keep.tile([P, PAIR * P], U8, name=name + "_plane", align_bytes=64)
            nc.vector.quantize_mx(out=codes[:].bitcast(FP8X4), scales=plane[:], in_=grouped[:])
            return [(codes[:, i * P : (i + 1) * P], plane[:, i * P : (i + 1) * P]) for i in range(PAIR)]

        def bank(number):
            return psum.tile([P, S], F32, name=f"bank{number}")

        def product(acc, weights, cols=WHOLE, start=True, stop=True):
            codes, plane = weights
            nc.tensor.matmul_mx(
                out=acc[:, cols],
                lhsT=codes.bitcast(FP8X4),
                lhsT_scale=plane,
                rhs=x_codes[:, cols].bitcast(FP8X4),
                rhs_scale=x_plane[:, cols],
                start=start,
                stop=stop,
            )
            return acc

        def negate(dst, src):
            nc.scalar.activation(dst, src, COPY, scale=-1.0)

        nc.vector.tensor_copy(picked[:], scale_win[:].indirect(offs_t[:]))
        for r in range(4):
            nc.sync.dma_start(x_plane[r:P:32, :].bitcast(I32), picked[16 + r : 32 : 4, :].bitcast(I32))
        w2_early = reuse.tile([P, PACK, N // 2], F32, name="w2_early", align_bytes=64, offset=0)
        w2_late = reuse.tile([P, PACK, N // 2], F32, name="w2_late", align_bytes=64, offset=4096)
        w2_rows = w2.rearrange("(p j) n -> p j n", j=PACK)
        nc.sync.dma_start(w2_early[:], w2_rows[:, :, 0 : N // 2])
        nc.sync.dma_start(w2_late[:], w2_rows[:, :, N // 2 : N])
        spread = keep.tile([P, 2, P], F32, name="spread", align_bytes=64)
        share = keep.tile([P, V], F32, name="share", align_bytes=64)
        rest = keep.tile([P, V], F32, name="rest", align_bytes=64)
        turned = bank(0)
        for c in range(2):
            nc.tensor.transpose(turned[:, c * P : (c + 1) * P], share_rows[:, c * P : (c + 1) * P], ident[:])
        nc.scalar.copy(
            spread[:].rearrange("p c (g r) -> p c g r", r=16),
            turned[:, 0:V].rearrange("p (c k o) -> p c k o", c=2, o=1)[:, :, 88:96, :].to_broadcast([P, 2, 8, 16]),
        )
        back = bank(1)
        for c in range(2):
            nc.tensor.transpose(back[:, c * P : (c + 1) * P], spread[:, c, :], ident[:])
        nc.scalar.copy(share[:], back[:, 0:V])
        nc.scalar.activation(rest[:], back[:, 0:V], COPY, bias=1.0, scale=-1.0)
        round_tiles(nc.vector.tensor_copy, w1_raw, 0, slice(0, 2), w1_bf)
        for t in range(2, TILES):
            round_tiles(negate, w1_raw, 0, slice(t, t + 1), w1_bf)
        q1 = quantize(w1_bf[0], "w1_lo") + quantize(w1_bf[1], "w1_hi")
        for cols in HALVES:
            nc.vector.tensor_copy(
                x_codes[:, cols], word_win[:].bitcast(U32).indirect(offs_t[:, cols.start // 16 : cols.stop // 16])
            )

        round_tiles(nc.scalar.copy, w2_early, 0, slice(PAIR, TILES), w2_bf)
        for t in range(PAIR):
            round_tiles(nc.vector.tensor_copy, w2_early, 0, slice(t, t + 1), w2_bf)
        y = [reuse.tile([P, S], F32, name=f"y{t}", align_bytes=64, offset=2048 * t) for t in range(PAIR)]
        out_t = out.rearrange("(a t i) s -> t a i s", t=TILES, i=2)

        def fetch(dst, rows):
            nc.scalar.activation(dst[:], rows[:].indirect(acc_t[:]), COPY)

        for half, cols in enumerate(HALVES):
            nc.scalar.copy(y[0][:, cols], product(bank(2 + half), q1[0], cols)[:, cols])
        nc.scalar.copy(y[1][:], product(bank(4), q1[1])[:])
        y2_bank = product(bank(5), q1[2])

        w2_codes = keep.tile([P, PAIR, P], U32, name="w2_codes", align_bytes=64)
        w2_plane = keep.tile([P, PAIR, P], U8, name="w2_plane", align_bytes=64)

        def quantize_half(t, half):
            cols = slice(half * P // 2, (half + 1) * P // 2)
            first = ((t % PAIR) * P + cols.start) * PACK
            nc.vector.quantize_mx(
                out=w2_codes[:, t, cols].bitcast(FP8X4),
                scales=w2_plane[:, t, cols],
                in_=w2_bf[t // PAIR][:, first : first + P // 2 * PACK],
            )

        for t in range(2):
            quantize_half(t, 0)
        for t in range(2):
            round_tiles(nc.vector.tensor_copy, w2_late, P // 2, slice(t, t + 1), w2_bf)
        for t in range(2):
            quantize_half(t, 1)
        round_tiles(nc.vector.tensor_copy, w2_late, P // 2, slice(2, TILES), w2_bf)
        y_found = {
            t: reuse.tile([P, V], F32, name=f"y_found{t}", align_bytes=64, offset=16384 + 1024 * t) for t in range(2)
        }
        nc.vector.tensor_tensor(y_found[0][:], y[0][:].indirect(acc_t[:]), rest[:], MULT)
        q2 = [(w2_codes[:, t, :], w2_plane[:, t, :]) for t in range(2)] + quantize(w2_bf[1], "w2_hi", offset=20480)
        nc.vector.tensor_tensor(y_found[1][:], y[1][:].indirect(acc_t[:]), rest[:], MULT)

        gap = [reuse.tile([P, S], F32, name=f"gap{t}", align_bytes=64, offset=8192 + 2048 * t) for t in range(TILES)]
        pull = [keep.tile([P, V], F32, name=f"pull{t}", align_bytes=64) for t in range(PAIR)]
        gap_found = keep.tile([P, PAIR, V], F32, name="gap_found", align_bytes=64)
        late_pull = keep.tile([P, PAIR, V], F32, name="late_pull", align_bytes=64)
        pull += [late_pull[:, i, :] for i in range(PAIR)]

        def gap_product(number, t):
            acc = product(bank(number), q2[t], stop=False)
            return product(acc, q1[t], start=False)

        def put(t):
            nc.vector.tensor_tensor(y[t][:].indirect(acc_t[:]), y_found[t][:], pull[t][:], ADD)
            nc.sync.dma_start(out_t[t], y[t][:])

        for t in range(PAIR):
            for half, cols in enumerate(HALVES):
                nc.scalar.copy(gap[t][:, cols], product(bank(6 - 6 * t + half), q2[t], cols)[:, cols])
        for t in range(PAIR):
            nc.vector.tensor_tensor(pull[t][:], gap[t][:].indirect(acc_t[:]), share[:], MULT)
        nc.scalar.copy(gap[2][:], gap_product(2, 2)[:])
        y3_bank = product(bank(6), q1[3], HALVES[0])
        nc.scalar.copy(gap[3][:], gap_product(3, 3)[:])
        product(y3_bank, q1[3], HALVES[1])
        mixed = reuse.tile([P, V], F32, name="mixed", align_bytes=64, offset=20480)
        nc.vector.tensor_tensor(mixed[:], y_found[0][:], pull[0][:], ADD)
        y.append(reuse.tile([P, S], F32, name="y2", align_bytes=64, offset=8192))
        negate(y[2][:], y2_bank[:])
        for t in range(PAIR, TILES):
            fetch(gap_found[:, t - PAIR, :], gap[t])
        for i in range(PAIR):
            nc.gpsimd.tensor_tensor(late_pull[:, i, :], gap_found[:, i, :], share[:], MULT)
        y_found[2] = reuse.tile([P, V], F32, name="y_found2", align_bytes=64, offset=14336)
        fetch(y_found[2], y[2])
        y.append(reuse.tile([P, S], F32, name="y3", align_bytes=64, offset=15360))
        negate(y[3][:], y3_bank[:])
        y_found[3] = keep.tile([P, V], F32, name="y_found3", align_bytes=64)
        fetch(y_found[3], y[3])
        put(1)
        nc.vector.tensor_copy(y[0][:].indirect(acc_t[:]), mixed[:])
        nc.sync.dma_start(out_t[0], y[0][:])
        for t in range(PAIR, TILES):
            put(t)
